import numpy as np
import ml_dtypes


def mxq(x, axis, fmt="e4m3"):
    dtype, down = {"e4m3": (ml_dtypes.float8_e4m3fn, 7), "e5m2": (ml_dtypes.float8_e5m2, 14)}[fmt]
    v = np.moveaxis(np.asarray(x, np.float32).astype(ml_dtypes.bfloat16).astype(np.float64), axis, -1)
    blocks = v.reshape(v.shape[:-1] + (-1, 32))
    amax = np.abs(blocks).max(-1, keepdims=True)
    byte = np.maximum(np.where(amax > 0, np.frexp(amax)[1] - 1 + 127, 0) - down, 1)
    scale = np.exp2(byte - 127.0)
    codes = (blocks / scale).astype(np.float32).astype(dtype).astype(np.float64)
    return np.moveaxis((codes * scale).reshape(v.shape), -1, axis)


WIDE = False


def mx_kscale(k):
    if not WIDE:
        return np.ones(k)
    levels = np.array([10, -10, 5, -5, 0])
    if k % 512:
        return np.exp2(np.random.permutation(np.resize(levels, k // 32))).repeat(32)
    a = np.empty((k // 512, 16))
    for p in range(k // 512):
        a[p, :8] = np.random.permutation(np.resize(levels, 8))
        for g in range(8):
            far = levels[np.abs(levels - a[p, g]) >= 10]
            a[p, g + 8] = far[np.random.randint(len(far))]
    return np.exp2(a.ravel()).repeat(32)


def f64(x):
    return np.asarray(x).astype(np.float64)


def striped(idx):
    return np.tile(idx.reshape(-1, 16).T, (8, 1)).astype(np.uint16)


def unstriped(offs):
    return offs[:16].T.reshape(-1).astype(np.int64)


E2M1 = np.array([0.0, 0.5, 1.0, 1.5, 2.0, 3.0, 4.0, 6.0, -0.0, -0.5, -1.0, -1.5, -2.0, -3.0, -4.0, -6.0])


def pack_weight(w, fmt):
    k, n = w.shape
    w = f64(np.asarray(w, np.float32).astype(ml_dtypes.bfloat16)).reshape(k // 32, 32, n)
    amax = np.abs(w).max(1)
    if fmt == "e4m3":
        byte = np.frexp(amax)[1] - 1 + 127 - 7
    else:
        mant, ex = np.frexp(amax / 6.0)
        byte = np.where(mant > 0.5, ex, ex - 1) + 127
    byte = np.clip(np.where(amax > 0, byte, 1), 1, 254)
    scaled = (w * np.exp2(127.0 - byte)[:, None, :]).reshape(k, n).astype(np.float32)
    by_word = np.ascontiguousarray(scaled.reshape(k // 512, 128, 4, n).transpose(0, 1, 3, 2))
    if fmt == "e4m3":
        words = by_word.astype(ml_dtypes.float8_e4m3fn).view(np.uint8)
    else:
        c = by_word.astype(ml_dtypes.float4_e2m1fn).view(np.uint8) & 0xF
        words = (c[..., 0::2] | (c[..., 1::2] << 4)).reshape(k // 512, 128, 2 * n)
    return np.ascontiguousarray(words), np.ascontiguousarray(byte.astype(np.uint8).reshape(k // 512, 16, n))


def unpack_weight(words, scales, fmt):
    g, _, n = scales.shape
    words = np.ascontiguousarray(words).reshape(g, 128, n, -1)
    if fmt == "e4m3":
        vals = words.view(ml_dtypes.float8_e4m3fn).astype(np.float64)
    else:
        nib = np.empty((g, 128, n, 4), np.uint8)
        nib[..., 0::2] = words & 0xF
        nib[..., 1::2] = words >> 4
        vals = E2M1[nib]
    vals = vals * np.repeat(np.exp2(scales.astype(np.float64) - 127.0), 8, axis=1)[..., None]
    return vals.transpose(0, 1, 3, 2).reshape(g * 512, n)


def gelu(v):
    return 0.5 * v * (1.0 + np.tanh(np.sqrt(2.0 / np.pi) * (v + 0.044715 * v**3)))


def bf(x):
    return np.asarray(x, np.float32).astype(ml_dtypes.bfloat16)

def planes(Y):
    n, m = Y.shape
    b = f64(bf(Y)).reshape(n // 32, 32, m)
    amax = np.abs(b).max(1)
    byte = np.clip(np.where(amax > 0, np.frexp(amax)[1] - 1 + 127 - 7, 1), 1, 254)
    codes = (b * np.exp2(127.0 - byte)[:, None, :]).reshape(n, m).astype(np.float32).astype(ml_dtypes.float8_e4m3fn).view(np.uint8)
    words = codes.reshape(n // 512, 128, 4, m).transpose(0, 1, 3, 2)
    return np.ascontiguousarray(words), np.ascontiguousarray(byte.astype(np.uint8).reshape(n // 512, 16, m))


K, KP, KT, T, S, H, N = 1536, 1024, 512, 4096, 1024, 1024, 512

def setup_inputs():
    n = np.random.standard_normal
    s = mx_kscale(K)[:, None]
    u = mx_kscale(H)[:, None]
    tab_words, tab_scales = pack_weight(n((K, T)) * s, "e4m3")
    wp = 0.6 * n((KP, H)) / np.sqrt(K) / s[:KP]
    wt_words, wt_scales = pack_weight(0.6 * n((KT, H)) / np.sqrt(K) / s[KP:], "e2m1")
    bh = 0.5 + 0.2 * n(H)
    gain = np.exp(0.3 * n(H)) * u[:, 0]
    w2 = 2.0 * n((H, N)) / np.sqrt(H) / u * np.exp(0.8 * n(N))
    offs = striped(np.random.permutation(T)[:S])
    return {"tab_words": tab_words, "tab_scales": tab_scales, "offs": offs,
            "wp": wp.astype(np.float32), "wt_words": wt_words, "wt_scales": wt_scales,
            "bh": bh.astype(np.float32), "gain": gain.astype(np.float32),
            "w2": w2.astype(np.float32)}

def reference(tab_words, tab_scales, offs, wp, wt_words, wt_scales, bh, gain, w2):
    v = unpack_weight(tab_words, tab_scales, "e4m3")[:, unstriped(offs)]
    wt = unpack_weight(wt_words, wt_scales, "e2m1")
    wpq = mxq(f64(wp), 0, "e4m3")
    a = (wpq.T @ v[:KP] + wt.T @ v[KP:]) + f64(bh)[:, None]
    c = np.minimum(np.maximum(a, 0.0), 1.0)
    h = np.square(c) * f64(gain)[:, None]
    y = mxq(f64(w2), 0, "e4m3").T @ mxq(h, 0, "e4m3")
    words, scales = planes(y)
    return y, words, scales

@@ -1,0 +1,273 @@
+from contextlib import ExitStack
+
+import concourse.mybir as mybir
+
+K, KP, KT, T, S, H, N = 1536, 1024, 512, 4096, 1024, 1024, 512
+FLOPS = 2 * K * H * S + 2 * H * N * S
+
+F32 = mybir.dt.float32
+BF16 = mybir.dt.bfloat16
+I32 = mybir.dt.int32
+U32 = mybir.dt.uint32
+U16 = mybir.dt.uint16
+U8 = mybir.dt.uint8
+E4M3 = mybir.dt.float8_e4m3fn_x4
+E2M1 = mybir.dt.float4_e2m1fn_x4
+ACT = mybir.ActivationFunctionType
+ALU = mybir.AluOpType
+
+P = 128
+PACK = 4
+PASS = P * PACK
+BANK = 512
+CHUNK = 256
+THREAT = 2
+SCALE_ROW = {THREAT: 0, 0: 4, 1: 8}
+VECTOR_M = 84
+
+
+def tile_list_chess_feature_value_kernel(
+    tc, tab_words, tab_scales, offs, wp, wt_words, wt_scales, bh, gain, w2, out_0, out_1, out_2
+):
+    nc = tc.nc
+    with ExitStack() as ctx:
+        keep = ctx.enter_context(tc.tile_pool(name="keep", bufs=1))
+        ring = ctx.enter_context(tc.tile_pool(name="ring", bufs=1))
+        psum = ctx.enter_context(tc.psum_pool(name="psum", bufs=8))
+
+        offsets = keep.tile([P, S // 16], U16, name="offsets")
+        nc.sync.dma_start(offsets[:], offs)
+
+        def slot(shape, dtype, name, tag):
+            return ring.tile(shape, dtype, name=name, tag=tag, bufs=1, align_bytes=64)
+
+        def load_table(a, tag):
+            words = slot([P, T], U32, "table%d" % a, tag)
+            nc.sync.dma_start(words[:].bitcast(I32), tab_words[a].rearrange("p t i -> p (t i)").bitcast(I32))
+            return words
+
+        def load_weight(rows, name, tag):
+            raw = slot([P, PACK, PASS], F32, name, tag)
+            nc.sync.dma_start(raw[:], rows.rearrange("(p j) c -> p j c", j=PACK))
+            return raw
+
+        def load_wp(g, a, tag):
+            return load_weight(wp[a * PASS : (a + 1) * PASS, g * PASS : (g + 1) * PASS], "raw_wp%d%d" % (g, a), tag)
+
+        def pick(a, words):
+            picked[a] = keep.tile([P, S], U32, name="picked%d" % a, align_bytes=64)
+            nc.vector.tensor_copy(picked[a][:], words[:].indirect(offsets[:]))
+
+        wt_raw = slot([P, 2 * H], U8, "wt_raw", "C")
+        nc.sync.dma_start(wt_raw[:].bitcast(I32), wt_words[0].bitcast(I32))
+        bias = keep.tile([P, 2, PACK], F32, name="bias")
+        nc.sync.dma_start(bias[:], bh.rearrange("(g p t) -> p g t", g=2, t=PACK))
+        gains = keep.tile([P, 2, PACK], F32, name="gains")
+        nc.sync.dma_start(gains[:], gain.rearrange("(g p t) -> p g t", g=2, t=PACK))
+        table_threat = load_table(THREAT, "A")
+        table_0 = load_table(0, "B")
+
+        table_scales = slot([P, T], U8, "table_scales", "D")
+        nc.vector.memset(table_scales[:].bitcast(I32), 0)
+        wt_scales_raw = keep.tile([P, H], U8, name="wt_scales_raw", align_bytes=64)
+        nc.gpsimd.memset(wt_scales_raw[:].bitcast(I32), 0)
+        for q in range(4):
+            (nc.sync if q < 2 else nc.gpsimd).dma_start(
+                wt_scales_raw[32 * q : 32 * q + 4, :].bitcast(I32), wt_scales[0, 4 * q : 4 * q + 4, :].bitcast(I32)
+            )
+        for q in range(4):
+            nc.sync.dma_start(
+                table_scales[32 * q : 32 * q + 4, :].bitcast(I32), tab_scales[THREAT, 4 * q : 4 * q + 4, :].bitcast(I32)
+            )
+        for q in range(4):
+            nc.gpsimd.dma_start(
+                table_scales[32 * q + 4 : 32 * q + 12, :].bitcast(I32), tab_scales[0:2, 4 * q : 4 * q + 4, :].bitcast(I32)
+            )
+
+        wt_dealt = keep.tile([P, 2 * H], U8, name="wt_dealt", align_bytes=64)
+        wt_plane = keep.tile([P, H], U8, name="wt_plane", align_bytes=64)
+        for g in range(2):
+            nc.vector.tensor_copy(
+                wt_dealt[:, 2 * g * PASS : 2 * (g + 1) * PASS].rearrange("p (t m b) -> p m t b", t=PACK, b=2),
+                wt_raw[:, 2 * g * PASS : 2 * (g + 1) * PASS].rearrange("p (m t b) -> p m t b", t=PACK, b=2),
+            )
+        raw_wp = {}
+        raw_wp[0, 0] = load_wp(0, 0, "C")
+
+        picked = {}
+        pick(THREAT, table_threat)
+        table_1 = load_table(1, "A")
+        pick(0, table_0)
+        raw_wp[0, 1] = load_wp(0, 1, "B")
+        picked_scales = keep.tile([P, S], U8, name="picked_scales", align_bytes=64)
+        nc.vector.tensor_copy(picked_scales[:], table_scales[:].indirect(offsets[:]))
+        nc.vector.tensor_copy(
+            wt_plane[:].rearrange("p (g t m) -> p g m t", g=2, t=PACK),
+            wt_scales_raw[:].rearrange("p (g m t) -> p g m t", g=2, t=PACK),
+        )
+
+        def round_weight(raw, name, shared):
+            dealt = ring.tile([P, PACK * PASS], BF16, name=name, tag="dealt", bufs=3, align_bytes=64)
+            dst = dealt[:].rearrange("p (t m j) -> p m t j", t=PACK, j=PACK)
+            src = raw[:].rearrange("p j (m t) -> p m t j", t=PACK)
+            if shared:
+                nc.vector.tensor_copy(dst[:, :VECTOR_M], src[:, :VECTOR_M])
+                nc.scalar.copy(dst[:, VECTOR_M:], src[:, VECTOR_M:])
+            else:
+                nc.vector.tensor_copy(dst, src)
+            return dealt
+
+        def quantize_weight(dealt, name, parts):
+            codes = keep.tile([P, PASS], U32, name=name + "_codes", align_bytes=64)
+            plane = keep.tile([P, PASS], U8, name=name + "_plane", align_bytes=64)
+            width = PASS // parts
+            for part in range(parts):
+                cols = slice(part * width, (part + 1) * width)
+                nc.vector.quantize_mx(
+                    out=codes[:, cols].bitcast(E4M3),
+                    scales=plane[:, cols],
+                    in_=dealt[:, PACK * cols.start : PACK * cols.stop],
+                )
+            return codes, plane
+
+        def first_pass(bank, g, t, half, a, weights, start, stop):
+            cols = slice(half * BANK, (half + 1) * BANK)
+            if a == THREAT:
+                c0 = g * PASS + t * P
+                lhs = wt_dealt[:, 2 * c0 : 2 * (c0 + P)].bitcast(E2M1)
+                lhs_scale = wt_plane[:, c0 : c0 + P]
+            else:
+                codes, plane = weights
+                lhs = codes[:, t * P : (t + 1) * P].bitcast(E4M3)
+                lhs_scale = plane[:, t * P : (t + 1) * P]
+            nc.tensor.matmul_mx(
+                out=bank[:],
+                lhsT=lhs,
+                lhsT_scale=lhs_scale,
+                rhs=picked[a][:, cols].bitcast(E4M3),
+                rhs_scale=picked_scales[SCALE_ROW[a] :, cols],
+                start=start,
+                stop=stop,
+            )
+
+        def rectify(g, half, banks, on_vector):
+            rectified = ring.tile([P, PACK, BANK], F32, name="rect%d%d" % (g, half), tag="rectified", bufs=2)
+            for t in range(PACK):
+                if t >= PACK - on_vector:
+                    nc.vector.tensor_scalar(rectified[:, t, :], banks[t][:], bias[:, g, t : t + 1], 0.0, ALU.add, ALU.max)
+                else:
+                    nc.scalar.activation(rectified[:, t, :], banks[t][:], ACT.Relu, bias=bias[:, g, t : t + 1])
+            return rectified
+
+        h_codes = [keep.tile([P, S], U32, name="h_codes%d" % g, align_bytes=64) for g in range(2)]
+        h_plane = [keep.tile([P, S], U8, name="h_plane%d" % g, align_bytes=64) for g in range(2)]
+
+        def finish_hidden(g, cols, rectified):
+            width = cols.stop - cols.start
+            c0 = cols.start % BANK
+            squared = ring.tile([P, width, PACK], F32, name="sq%d_%d" % (g, cols.start), tag="squared", bufs=3)
+            nc.scalar.activation(
+                squared[:].rearrange("p (c i) t -> p c t i", i=4),
+                rectified[:, :, c0 : c0 + width].rearrange("p t (c i) -> p c t i", i=4),
+                ACT.Square,
+            )
+            hidden = ring.tile([P, width, PACK], BF16, name="hid%d_%d" % (g, cols.start), tag="hidden", bufs=3, align_bytes=64)
+            nc.vector.scalar_tensor_tensor(
+                hidden[:],
+                squared[:],
+                1.0,
+                gains[:, g : g + 1, :].to_broadcast([P, width, PACK]),
+                ALU.min,
+                ALU.mult,
+            )
+            nc.vector.quantize_mx(
+                out=h_codes[g][:, cols].bitcast(E4M3),
+                scales=h_plane[g][:, cols],
+                in_=hidden[:].rearrange("p n t -> p (n t)"),
+            )
+
+        y_codes = keep.tile([P, S], U32, name="y_codes", align_bytes=64)
+        y_plane = keep.tile([P, S], U8, name="y_plane", align_bytes=64)
+        y_rows = out_0.rearrange("(p t) j -> p t j", t=PACK)
+        y_words = out_1[0].rearrange("p m t -> p (m t)").bitcast(I32)
+
+        def second_stage(cols, w2_mx):
+            width = cols.stop - cols.start
+            side = BANK // width
+            banks = [psum.tile([P, BANK], F32, name="ybank%d_%d" % (cols.start, b), tag="bank") for b in range(PACK // side)]
+            for g in range(2):
+                codes, plane = w2_mx[g]
+                for t in range(PACK):
+                    nc.tensor.matmul_mx(
+                        out=banks[t // side][:, (t % side) * width : (t % side + 1) * width],
+                        lhsT=codes[:, t * P : (t + 1) * P].bitcast(E4M3),
+                        lhsT_scale=plane[:, t * P : (t + 1) * P],
+                        rhs=h_codes[g][:, cols].bitcast(E4M3),
+                        rhs_scale=h_plane[g][:, cols],
+                        start=(g == 0 and t % side == 0),
+                        stop=(g == 1 and t % side == side - 1),
+                    )
+            y = ring.tile([P, PACK, width], F32, name="y%d" % cols.start, tag="y", bufs=5)
+            for b in range(PACK // side):
+                dst = y[:, b * side : (b + 1) * side, :].rearrange("p t n -> p (t n)")
+                nc.scalar.copy(dst, banks[b][:])
+            nc.sync.dma_start(y_rows[:, :, cols], y[:])
+            rounded = ring.tile([P, width, PACK], BF16, name="yb%d" % cols.start, tag="rounded", bufs=2, align_bytes=64)
+            nc.vector.tensor_copy(
+                rounded[:].rearrange("p (c i) t -> p c t i", i=4), y[:].rearrange("p t (c i) -> p c t i", i=4)
+            )
+            nc.vector.quantize_mx(
+                out=y_codes[:, cols].bitcast(E4M3), scales=y_plane[:, cols], in_=rounded[:].rearrange("p n t -> p (n t)")
+            )
+            nc.sync.dma_start(y_words[:, cols], y_codes[:, cols].bitcast(I32))
+
+        def open_banks(g, half):
+            return [psum.tile([P, BANK], F32, name="bank%d%d%d" % (g, half, t), tag="bank") for t in range(PACK)]
+
+        banks0 = [open_banks(0, half) for half in range(2)]
+        for half in range(2):
+            for t in range(PACK):
+                first_pass(banks0[half][t], 0, t, half, THREAT, None, True, False)
+        weights = quantize_weight(round_weight(raw_wp[0, 0], "wp00", True), "wp00", 1)
+        raw_wp[1, 0] = load_wp(1, 0, "C")
+        raw_wp[1, 1] = load_wp(1, 1, "D")
+        for half in range(2):
+            for t in range(PACK):
+                first_pass(banks0[half][t], 0, t, half, 0, weights, False, False)
+        pick(1, table_1)
+        weights = quantize_weight(round_weight(raw_wp[0, 1], "wp01", True), "wp01", PACK)
+        raw_w2 = [load_weight(w2[0:PASS, :], "raw_w20", "B")]
+        for half in range(2):
+            for t in range(PACK):
+                first_pass(banks0[half][t], 0, t, half, 1, weights, False, True)
+        rect = rectify(0, 0, banks0[0], 2)
+        wp1 = [quantize_weight(round_weight(raw_wp[1, 0], "wp10", False), "wp10", 1)]
+        raw_w2.append(load_weight(w2[PASS : 2 * PASS, :], "raw_w21", "C"))
+        finish_hidden(0, slice(0, 256), rect)
+        finish_hidden(0, slice(256, 512), rect)
+        wp1.append(quantize_weight(round_weight(raw_wp[1, 1], "wp11", False), "wp11", 1))
+        rect = rectify(0, 1, banks0[1], 0)
+        finish_hidden(0, slice(512, 1024), rect)
+        banks1 = []
+        for half in range(2):
+            banks1.append(open_banks(1, half))
+            for t in range(PACK):
+                for a in (THREAT, 0, 1):
+                    first_pass(banks1[half][t], 1, t, half, a, None if a == THREAT else wp1[a], a == THREAT, a == 1)
+        w2_mx = [quantize_weight(round_weight(raw_w2[g], "w2%d" % g, False), "w2%d" % g, 1) for g in range(2)]
+        rect = rectify(1, 0, banks1[0], 0)
+        chunks = [slice(0, 256), slice(256, 512), slice(512, 768), slice(768, 896), slice(896, 1024)]
+        finish_hidden(1, chunks[0], rect)
+        finish_hidden(1, chunks[1], rect)
+        rect = rectify(1, 1, banks1[1], 0)
+        second_stage(chunks[0], w2_mx)
+        finish_hidden(1, chunks[2], rect)
+        second_stage(chunks[1], w2_mx)
+        finish_hidden(1, chunks[3], rect)
+        finish_hidden(1, chunks[4], rect)
+        for cols in chunks[2:]:
+            second_stage(cols, w2_mx)
+        for q in range(4):
+            (nc.sync if q < 2 else nc.scalar).dma_start(
+                out_2[0, 4 * q : 4 * q + 4, :].bitcast(I32), y_plane[32 * q : 32 * q + 4, :].bitcast(I32)
+            )

@@ -54,34 +54,40 @@ def tile_list_chess_feature_value_kernel(
         def load_wp(g, a, tag):
             return load_weight(wp[a * PASS : (a + 1) * PASS, g * PASS : (g + 1) * PASS], "raw_wp%d%d" % (g, a), tag)
 
-        def pick(a, words):
+        def pick(a, words, parts=1):
             picked[a] = keep.tile([P, S], U32, name="picked%d" % a, align_bytes=64)
-            nc.vector.tensor_copy(picked[a][:], words[:].indirect(offsets[:]))
+            width = S // parts
+            for c0 in range(0, S, width):
+                nc.vector.tensor_copy(
+                    picked[a][:, c0 : c0 + width], words[:].indirect(offsets[:, c0 // 16 : (c0 + width) // 16])
+                )
 
-        wt_raw = slot([P, 2 * H], U8, "wt_raw", "C")
-        nc.sync.dma_start(wt_raw[:].bitcast(I32), wt_words[0].bitcast(I32))
+        wt_raw = [slot([P, 2 * PASS], U8, "wt_raw%d" % g, "CE"[g]) for g in range(2)]
+        for g in range(2):
+            nc.sync.dma_start(wt_raw[g][:].bitcast(I32), wt_words[0, :, 2 * g * PASS : 2 * (g + 1) * PASS].bitcast(I32))
         bias = keep.tile([P, 2, PACK], F32, name="bias")
         nc.sync.dma_start(bias[:], bh.rearrange("(g p t) -> p g t", g=2, t=PACK))
         gains = keep.tile([P, 2, PACK], F32, name="gains")
         nc.sync.dma_start(gains[:], gain.rearrange("(g p t) -> p g t", g=2, t=PACK))
-        table_threat = load_table(THREAT, "A")
-        table_0 = load_table(0, "B")
+        table_0 = load_table(0, "A")
+        raw_wp = {}
+        raw_wp[0, 0] = load_wp(0, 0, "B")
 
         table_scales = slot([P, T], U8, "table_scales", "D")
         nc.vector.memset(table_scales[:].bitcast(I32), 0)
         wt_scales_raw = keep.tile([P, H], U8, name="wt_scales_raw", align_bytes=64)
-        nc.gpsimd.memset(wt_scales_raw[:].bitcast(I32), 0)
+        nc.vector.memset(wt_scales_raw[:].bitcast(I32), 0)
         for q in range(4):
-            (nc.sync if q < 2 else nc.gpsimd).dma_start(
-                wt_scales_raw[32 * q : 32 * q + 4, :].bitcast(I32), wt_scales[0, 4 * q : 4 * q + 4, :].bitcast(I32)
+            (nc.gpsimd if q < 3 else nc.sync).dma_start(
+                table_scales[32 * q + 4 : 32 * q + 12, :].bitcast(I32), tab_scales[0:2, 4 * q : 4 * q + 4, :].bitcast(I32)
             )
         for q in range(4):
             nc.sync.dma_start(
                 table_scales[32 * q : 32 * q + 4, :].bitcast(I32), tab_scales[THREAT, 4 * q : 4 * q + 4, :].bitcast(I32)
             )
         for q in range(4):
-            nc.gpsimd.dma_start(
-                table_scales[32 * q + 4 : 32 * q + 12, :].bitcast(I32), tab_scales[0:2, 4 * q : 4 * q + 4, :].bitcast(I32)
+            (nc.sync if q < 1 else nc.gpsimd).dma_start(
+                wt_scales_raw[32 * q : 32 * q + 4, :].bitcast(I32), wt_scales[0, 4 * q : 4 * q + 4, :].bitcast(I32)
             )
 
         wt_dealt = keep.tile([P, 2 * H], U8, name="wt_dealt", align_bytes=64)
@@ -89,30 +95,23 @@ def tile_list_chess_feature_value_kernel(
         for g in range(2):
             nc.vector.tensor_copy(
                 wt_dealt[:, 2 * g * PASS : 2 * (g + 1) * PASS].rearrange("p (t m b) -> p m t b", t=PACK, b=2),
-                wt_raw[:, 2 * g * PASS : 2 * (g + 1) * PASS].rearrange("p (m t b) -> p m t b", t=PACK, b=2),
+                wt_raw[g][:].rearrange("p (m t b) -> p m t b", t=PACK, b=2),
             )
-        raw_wp = {}
-        raw_wp[0, 0] = load_wp(0, 0, "C")
+        table_threat = load_table(THREAT, "C")
+        raw_wp[0, 1] = load_wp(0, 1, "E")
 
         picked = {}
-        pick(THREAT, table_threat)
-        table_1 = load_table(1, "A")
         pick(0, table_0)
-        raw_wp[0, 1] = load_wp(0, 1, "B")
         picked_scales = keep.tile([P, S], U8, name="picked_scales", align_bytes=64)
         nc.vector.tensor_copy(picked_scales[:], table_scales[:].indirect(offsets[:]))
-        nc.vector.tensor_copy(
-            wt_plane[:].rearrange("p (g t m) -> p g m t", g=2, t=PACK),
-            wt_scales_raw[:].rearrange("p (g m t) -> p g m t", g=2, t=PACK),
-        )
+        table_1 = load_table(1, "D")
 
-        def round_weight(raw, name, shared):
-            dealt = ring.tile([P, PACK * PASS], BF16, name=name, tag="dealt", bufs=3, align_bytes=64)
+        def round_weight(raw, name, shared, tag):
+            dealt = slot([P, PACK * PASS], BF16, name, tag)
             dst = dealt[:].rearrange("p (t m j) -> p m t j", t=PACK, j=PACK)
             src = raw[:].rearrange("p j (m t) -> p m t j", t=PACK)
             if shared:
-                nc.vector.tensor_copy(dst[:, :VECTOR_M], src[:, :VECTOR_M])
-                nc.scalar.copy(dst[:, VECTOR_M:], src[:, VECTOR_M:])
+                nc.scalar.copy(dst, src)
             else:
                 nc.vector.tensor_copy(dst, src)
             return dealt
@@ -151,7 +150,7 @@ def tile_list_chess_feature_value_kernel(
             )
 
         def rectify(g, half, banks, on_vector):
-            rectified = ring.tile([P, PACK, BANK], F32, name="rect%d%d" % (g, half), tag="rectified", bufs=2)
+            rectified = ring.tile([P, PACK, BANK], F32, name="rect%d%d" % (g, half), tag="rectified", bufs=3)
             for t in range(PACK):
                 if t >= PACK - on_vector:
                     nc.vector.tensor_scalar(rectified[:, t, :], banks[t][:], bias[:, g, t : t + 1], 0.0, ALU.add, ALU.max)
@@ -162,10 +161,13 @@ def tile_list_chess_feature_value_kernel(
         h_codes = [keep.tile([P, S], U32, name="h_codes%d" % g, align_bytes=64) for g in range(2)]
         h_plane = [keep.tile([P, S], U8, name="h_plane%d" % g, align_bytes=64) for g in range(2)]
 
-        def finish_hidden(g, cols, rectified):
+        def finish_hidden(g, cols, rectified, tag=None):
             width = cols.stop - cols.start
             c0 = cols.start % BANK
-            squared = ring.tile([P, width, PACK], F32, name="sq%d_%d" % (g, cols.start), tag="squared", bufs=3)
+            if tag is None:
+                squared = ring.tile([P, width, PACK], F32, name="sq%d_%d" % (g, cols.start), tag="squared", bufs=4)
+            else:
+                squared = slot([P, width, PACK], F32, "sq%d_%d" % (g, cols.start), tag)
             nc.scalar.activation(
                 squared[:].rearrange("p (c i) t -> p c t i", i=4),
                 rectified[:, :, c0 : c0 + width].rearrange("p t (c i) -> p c t i", i=4),
@@ -191,7 +193,7 @@ def tile_list_chess_feature_value_kernel(
         y_rows = out_0.rearrange("(p t) j -> p t j", t=PACK)
         y_words = out_1[0].rearrange("p m t -> p (m t)").bitcast(I32)
 
-        def second_stage(cols, w2_mx):
+        def second_stage(cols, w2_mx, last_on_vector=False):
             width = cols.stop - cols.start
             side = BANK // width
             banks = [psum.tile([P, BANK], F32, name="ybank%d_%d" % (cols.start, b), tag="bank") for b in range(PACK // side)]
@@ -210,8 +212,15 @@ def tile_list_chess_feature_value_kernel(
             y = ring.tile([P, PACK, width], F32, name="y%d" % cols.start, tag="y", bufs=5)
             for b in range(PACK // side):
                 dst = y[:, b * side : (b + 1) * side, :].rearrange("p t n -> p (t n)")
-                nc.scalar.copy(dst, banks[b][:])
+                if last_on_vector and b == len(banks) - 1:
+                    nc.vector.tensor_copy(dst, banks[b][:])
+                else:
+                    nc.scalar.copy(dst, banks[b][:])
             nc.sync.dma_start(y_rows[:, :, cols], y[:])
+            return y
+
+        def quantize_y(cols, y):
+            width = cols.stop - cols.start
             rounded = ring.tile([P, width, PACK], BF16, name="yb%d" % cols.start, tag="rounded", bufs=2, align_bytes=64)
             nc.vector.tensor_copy(
                 rounded[:].rearrange("p (c i) t -> p c t i", i=4), y[:].rearrange("p t (c i) -> p c t i", i=4)
@@ -219,54 +228,62 @@ def tile_list_chess_feature_value_kernel(
             nc.vector.quantize_mx(
                 out=y_codes[:, cols].bitcast(E4M3), scales=y_plane[:, cols], in_=rounded[:].rearrange("p n t -> p (n t)")
             )
+
+        def store_codes(cols):
             nc.sync.dma_start(y_words[:, cols], y_codes[:, cols].bitcast(I32))
 
         def open_banks(g, half):
             return [psum.tile([P, BANK], F32, name="bank%d%d%d" % (g, half, t), tag="bank") for t in range(PACK)]
 
         banks0 = [open_banks(0, half) for half in range(2)]
+        weights = quantize_weight(round_weight(raw_wp[0, 0], "wp00", True, "H"), "wp00", 1)
         for half in range(2):
             for t in range(PACK):
-                first_pass(banks0[half][t], 0, t, half, THREAT, None, True, False)
-        weights = quantize_weight(round_weight(raw_wp[0, 0], "wp00", True), "wp00", 1)
+                first_pass(banks0[half][t], 0, t, half, 0, weights, True, False)
+        pick(THREAT, table_threat)
+        nc.vector.tensor_copy(
+            wt_plane[:].rearrange("p (g t m) -> p g m t", g=2, t=PACK),
+            wt_scales_raw[:].rearrange("p (g m t) -> p g m t", g=2, t=PACK),
+        )
+        for half in range(2):
+            for t in range(PACK):
+                first_pass(banks0[half][t], 0, t, half, THREAT, None, False, False)
         raw_wp[1, 0] = load_wp(1, 0, "C")
-        raw_wp[1, 1] = load_wp(1, 1, "D")
-        for half in range(2):
-            for t in range(PACK):
-                first_pass(banks0[half][t], 0, t, half, 0, weights, False, False)
-        pick(1, table_1)
-        weights = quantize_weight(round_weight(raw_wp[0, 1], "wp01", True), "wp01", PACK)
-        raw_w2 = [load_weight(w2[0:PASS, :], "raw_w20", "B")]
+        weights = quantize_weight(round_weight(raw_wp[0, 1], "wp01", True, "I"), "wp01", 1)
+        raw_wp[1, 1] = load_wp(1, 1, "E")
+        pick(1, table_1, 2)
         for half in range(2):
             for t in range(PACK):
                 first_pass(banks0[half][t], 0, t, half, 1, weights, False, True)
-        rect = rectify(0, 0, banks0[0], 2)
-        wp1 = [quantize_weight(round_weight(raw_wp[1, 0], "wp10", False), "wp10", 1)]
-        raw_w2.append(load_weight(w2[PASS : 2 * PASS, :], "raw_w21", "C"))
-        finish_hidden(0, slice(0, 256), rect)
-        finish_hidden(0, slice(256, 512), rect)
-        wp1.append(quantize_weight(round_weight(raw_wp[1, 1], "wp11", False), "wp11", 1))
-        rect = rectify(0, 1, banks0[1], 0)
-        finish_hidden(0, slice(512, 1024), rect)
+        chunks = [slice(0, 256), slice(256, 512), slice(512, 768), slice(768, 896), slice(896, 1024)]
+        rect00 = rectify(0, 0, banks0[0], 0)
+        wp1 = [quantize_weight(round_weight(raw_wp[1, a], "wp1%d" % a, False, "D"), "wp1%d" % a, 1) for a in range(2)]
+        raw_w2 = [load_weight(w2[g * PASS : (g + 1) * PASS, :], "raw_w2%d" % g, "IC"[g]) for g in range(2)]
+        finish_hidden(0, chunks[0], rect00, "F")
+        finish_hidden(0, chunks[1], rect00, "G")
+        rect01 = rectify(0, 1, banks0[1], 0)
         banks1 = []
         for half in range(2):
             banks1.append(open_banks(1, half))
             for t in range(PACK):
                 for a in (THREAT, 0, 1):
                     first_pass(banks1[half][t], 1, t, half, a, None if a == THREAT else wp1[a], a == THREAT, a == 1)
-        w2_mx = [quantize_weight(round_weight(raw_w2[g], "w2%d" % g, False), "w2%d" % g, 1) for g in range(2)]
-        rect = rectify(1, 0, banks1[0], 0)
-        chunks = [slice(0, 256), slice(256, 512), slice(512, 768), slice(768, 896), slice(896, 1024)]
-        finish_hidden(1, chunks[0], rect)
-        finish_hidden(1, chunks[1], rect)
-        rect = rectify(1, 1, banks1[1], 0)
-        second_stage(chunks[0], w2_mx)
-        finish_hidden(1, chunks[2], rect)
-        second_stage(chunks[1], w2_mx)
-        finish_hidden(1, chunks[3], rect)
-        finish_hidden(1, chunks[4], rect)
+        w2_mx = [quantize_weight(round_weight(raw_w2[g], "w2%d" % g, False, "FG"[g]), "w2%d" % g, 1) for g in range(2)]
+        rect10 = rectify(1, 0, banks1[0], 0)
+        finish_hidden(1, chunks[0], rect10)
+        finish_hidden(1, chunks[1], rect10)
+        ys = [second_stage(cols, w2_mx) for cols in chunks[:2]]
+        finish_hidden(0, slice(512, 768), rect01)
+        finish_hidden(0, slice(768, 1024), rect01)
+        rect11 = rectify(1, 1, banks1[1], 0)
         for cols in chunks[2:]:
-            second_stage(cols, w2_mx)
+            finish_hidden(1, cols, rect11)
+        for cols in chunks[2:]:
+            ys.append(second_stage(cols, w2_mx, cols.start != 768))
+        for cols, y in zip(chunks, ys):
+            quantize_y(cols, y)
+            if cols.stop in (512, 768, 1024):
+                store_codes(slice({512: 0, 768: 512, 1024: 768}[cols.stop], cols.stop))
         for q in range(4):
             (nc.sync if q < 2 else nc.scalar).dma_start(
                 out_2[0, 4 * q : 4 * q + 4, :].bitcast(I32), y_plane[32 * q : 32 * q + 4, :].bitcast(I32)

@@ -104,12 +104,11 @@ def tile_list_chess_feature_value_kernel(
         pick(0, table_0)
         picked_scales = keep.tile([P, S], U8, name="picked_scales", align_bytes=64)
         nc.vector.tensor_copy(picked_scales[:], table_scales[:].indirect(offsets[:]))
-        table_1 = load_table(1, "D")
 
         def round_weight(raw, name, shared, tag):
             dealt = slot([P, PACK * PASS], BF16, name, tag)
-            dst = dealt[:].rearrange("p (t m j) -> p m t j", t=PACK, j=PACK)
-            src = raw[:].rearrange("p j (m t) -> p m t j", t=PACK)
+            dst = dealt[:].rearrange("p (t m j) -> p m j t", t=PACK, j=PACK)
+            src = raw[:].rearrange("p j (m t) -> p m j t", t=PACK)
             if shared:
                 nc.scalar.copy(dst, src)
             else:
@@ -173,7 +172,7 @@ def tile_list_chess_feature_value_kernel(
                 rectified[:, :, c0 : c0 + width].rearrange("p t (c i) -> p c t i", i=4),
                 ACT.Square,
             )
-            hidden = ring.tile([P, width, PACK], BF16, name="hid%d_%d" % (g, cols.start), tag="hidden", bufs=3, align_bytes=64)
+            hidden = ring.tile([P, width, PACK], BF16, name="hid%d_%d" % (g, cols.start), tag="hidden", bufs=4, align_bytes=64)
             nc.vector.scalar_tensor_tensor(
                 hidden[:],
                 squared[:],
@@ -182,6 +181,9 @@ def tile_list_chess_feature_value_kernel(
                 ALU.min,
                 ALU.mult,
             )
+            return hidden
+
+        def quantize_hidden(g, cols, hidden):
             nc.vector.quantize_mx(
                 out=h_codes[g][:, cols].bitcast(E4M3),
                 scales=h_plane[g][:, cols],
@@ -219,12 +221,15 @@ def tile_list_chess_feature_value_kernel(
             nc.sync.dma_start(y_rows[:, :, cols], y[:])
             return y
 
-        def quantize_y(cols, y):
+        def round_y(cols, y):
             width = cols.stop - cols.start
-            rounded = ring.tile([P, width, PACK], BF16, name="yb%d" % cols.start, tag="rounded", bufs=2, align_bytes=64)
+            rounded = ring.tile([P, width, PACK], BF16, name="yb%d" % cols.start, tag="rounded", bufs=3, align_bytes=64)
             nc.vector.tensor_copy(
                 rounded[:].rearrange("p (c i) t -> p c t i", i=4), y[:].rearrange("p t (c i) -> p c t i", i=4)
             )
+            return rounded
+
+        def quantize_y(cols, rounded):
             nc.vector.quantize_mx(
                 out=y_codes[:, cols].bitcast(E4M3), scales=y_plane[:, cols], in_=rounded[:].rearrange("p n t -> p (n t)")
             )
@@ -237,6 +242,7 @@ def tile_list_chess_feature_value_kernel(
 
         banks0 = [open_banks(0, half) for half in range(2)]
         weights = quantize_weight(round_weight(raw_wp[0, 0], "wp00", True, "H"), "wp00", 1)
+        table_1 = load_table(1, "B")
         for half in range(2):
             for t in range(PACK):
                 first_pass(banks0[half][t], 0, t, half, 0, weights, True, False)
@@ -256,11 +262,17 @@ def tile_list_chess_feature_value_kernel(
             for t in range(PACK):
                 first_pass(banks0[half][t], 0, t, half, 1, weights, False, True)
         chunks = [slice(0, 256), slice(256, 512), slice(512, 768), slice(768, 896), slice(896, 1024)]
+        c0, c1, c2, c3, c4 = chunks
+        late = slice(768, 1024)
         rect00 = rectify(0, 0, banks0[0], 0)
-        wp1 = [quantize_weight(round_weight(raw_wp[1, a], "wp1%d" % a, False, "D"), "wp1%d" % a, 1) for a in range(2)]
+        dealt = round_weight(raw_wp[1, 0], "wp10", False, "B")
         raw_w2 = [load_weight(w2[g * PASS : (g + 1) * PASS, :], "raw_w2%d" % g, "IC"[g]) for g in range(2)]
-        finish_hidden(0, chunks[0], rect00, "F")
-        finish_hidden(0, chunks[1], rect00, "G")
+        h00 = finish_hidden(0, c0, rect00, "F")
+        wp1 = [quantize_weight(dealt, "wp10", 1)]
+        dealt = round_weight(raw_wp[1, 1], "wp11", False, "B")
+        quantize_hidden(0, c0, h00)
+        wp1.append(quantize_weight(dealt, "wp11", 1))
+        h01 = finish_hidden(0, c1, rect00, "G")
         rect01 = rectify(0, 1, banks0[1], 0)
         banks1 = []
         for half in range(2):
@@ -268,22 +280,45 @@ def tile_list_chess_feature_value_kernel(
             for t in range(PACK):
                 for a in (THREAT, 0, 1):
                     first_pass(banks1[half][t], 1, t, half, a, None if a == THREAT else wp1[a], a == THREAT, a == 1)
-        w2_mx = [quantize_weight(round_weight(raw_w2[g], "w2%d" % g, False, "FG"[g]), "w2%d" % g, 1) for g in range(2)]
+        dealt0 = round_weight(raw_w2[0], "w20", False, "F")
+        quantize_hidden(0, c1, h01)
+        dealt1 = round_weight(raw_w2[1], "w21", False, "G")
+        w2_mx = [quantize_weight(dealt0, "w20", 1)]
         rect10 = rectify(1, 0, banks1[0], 0)
-        finish_hidden(1, chunks[0], rect10)
-        finish_hidden(1, chunks[1], rect10)
-        ys = [second_stage(cols, w2_mx) for cols in chunks[:2]]
-        finish_hidden(0, slice(512, 768), rect01)
-        finish_hidden(0, slice(768, 1024), rect01)
+        h10 = finish_hidden(1, c0, rect10)
+        w2_mx.append(quantize_weight(dealt1, "w21", 1))
+        h11 = finish_hidden(1, c1, rect10)
+        quantize_hidden(1, c0, h10)
+        y0 = second_stage(c0, w2_mx)
+        h02 = finish_hidden(0, c2, rect01)
+        quantize_hidden(1, c1, h11)
+        y1 = second_stage(c1, w2_mx)
+        h03 = finish_hidden(0, late, rect01)
+        quantize_hidden(0, c2, h02)
+        r0 = round_y(c0, y0)
+        quantize_hidden(0, late, h03)
         rect11 = rectify(1, 1, banks1[1], 0)
-        for cols in chunks[2:]:
-            finish_hidden(1, cols, rect11)
-        for cols in chunks[2:]:
-            ys.append(second_stage(cols, w2_mx, cols.start != 768))
-        for cols, y in zip(chunks, ys):
-            quantize_y(cols, y)
-            if cols.stop in (512, 768, 1024):
-                store_codes(slice({512: 0, 768: 512, 1024: 768}[cols.stop], cols.stop))
+        h12 = finish_hidden(1, c2, rect11)
+        quantize_y(c0, r0)
+        h13 = finish_hidden(1, c3, rect11)
+        quantize_hidden(1, c2, h12)
+        y2 = second_stage(c2, w2_mx)
+        h14 = finish_hidden(1, c4, rect11)
+        quantize_hidden(1, c3, h13)
+        y3 = second_stage(c3, w2_mx)
+        r1 = round_y(c1, y1)
+        quantize_hidden(1, c4, h14)
+        y4 = second_stage(c4, w2_mx)
+        r2 = round_y(c2, y2)
+        quantize_y(c1, r1)
+        store_codes(slice(0, 512))
+        r3 = round_y(c3, y3)
+        quantize_y(c2, r2)
+        store_codes(c2)
+        r4 = round_y(c4, y4)
+        quantize_y(c3, r3)
+        quantize_y(c4, r4)
+        store_codes(late)
         for q in range(4):
             (nc.sync if q < 2 else nc.scalar).dma_start(
                 out_2[0, 4 * q : 4 * q + 4, :].bitcast(I32), y_plane[32 * q : 32 * q + 4, :].bitcast(I32)

@@ -90,6 +90,22 @@ def tile_list_chess_feature_value_kernel(
                 wt_scales_raw[32 * q : 32 * q + 4, :].bitcast(I32), wt_scales[0, 4 * q : 4 * q + 4, :].bitcast(I32)
             )
 
+        magnitude = keep.tile([P, 2 * PACK], F32, name="magnitude")
+        nc.scalar.activation(magnitude[:], gains[:].rearrange("p g t -> p (g t)"), ACT.Abs)
+        rough = keep.tile([P, 2 * PACK], F32, name="rough")
+        nc.scalar.activation(rough[:], magnitude[:], ACT.Sqrt)
+        inverse = keep.tile([P, 2 * PACK], F32, name="inverse")
+        nc.vector.tensor_scalar(inverse[:], rough[:], 1e-30, None, ALU.max)
+        nc.vector.reciprocal(inverse[:], inverse[:])
+        nc.vector.tensor_tensor(inverse[:], inverse[:], magnitude[:], ALU.mult)
+        nc.vector.tensor_tensor(inverse[:], inverse[:], rough[:], ALU.add)
+        root = keep.tile([P, 2 * PACK], F32, name="root")
+        nc.vector.tensor_scalar(root[:], inverse[:], 0.5, None, ALU.mult)
+        positive = keep.tile([P, 2, PACK], F32, name="positive")
+        nc.vector.tensor_scalar(positive[:], gains[:], 0.0, None, ALU.is_ge)
+        signs = keep.tile([P, 2, PACK], BF16, name="signs")
+        nc.vector.tensor_scalar(signs[:], positive[:], 2.0, -1.0, ALU.mult, ALU.add)
+
         wt_dealt = keep.tile([P, 2 * H], U8, name="wt_dealt", align_bytes=64)
         wt_plane = keep.tile([P, H], U8, name="wt_plane", align_bytes=64)
         for g in range(2):
@@ -151,10 +167,15 @@ def tile_list_chess_feature_value_kernel(
         def rectify(g, half, banks, on_vector):
             rectified = ring.tile([P, PACK, BANK], F32, name="rect%d%d" % (g, half), tag="rectified", bufs=3)
             for t in range(PACK):
-                if t >= PACK - on_vector:
+                if t < on_vector:
                     nc.vector.tensor_scalar(rectified[:, t, :], banks[t][:], bias[:, g, t : t + 1], 0.0, ALU.add, ALU.max)
                 else:
                     nc.scalar.activation(rectified[:, t, :], banks[t][:], ACT.Relu, bias=bias[:, g, t : t + 1])
+            for t in list(range(on_vector, PACK)) + list(range(on_vector)):
+                column = g * PACK + t
+                nc.vector.tensor_scalar(
+                    rectified[:, t, :], rectified[:, t, :], 1.0, root[:, column : column + 1], ALU.min, ALU.mult
+                )
             return rectified
 
         h_codes = [keep.tile([P, S], U32, name="h_codes%d" % g, align_bytes=64) for g in range(2)]
@@ -163,25 +184,27 @@ def tile_list_chess_feature_value_kernel(
         def finish_hidden(g, cols, rectified, tag=None):
             width = cols.stop - cols.start
             c0 = cols.start % BANK
+            name = "hid%d_%d" % (g, cols.start)
             if tag is None:
-                squared = ring.tile([P, width, PACK], F32, name="sq%d_%d" % (g, cols.start), tag="squared", bufs=4)
+                hidden = ring.tile([P, width, PACK], BF16, name=name, tag="hidden", bufs=4, align_bytes=64)
             else:
-                squared = slot([P, width, PACK], F32, "sq%d_%d" % (g, cols.start), tag)
+                hidden = slot([P, width, PACK], BF16, name, tag)
             nc.scalar.activation(
-                squared[:].rearrange("p (c i) t -> p c t i", i=4),
+                hidden[:].rearrange("p (c i) t -> p c t i", i=4),
                 rectified[:, :, c0 : c0 + width].rearrange("p t (c i) -> p c t i", i=4),
                 ACT.Square,
             )
-            hidden = ring.tile([P, width, PACK], BF16, name="hid%d_%d" % (g, cols.start), tag="hidden", bufs=4, align_bytes=64)
-            nc.vector.scalar_tensor_tensor(
-                hidden[:],
-                squared[:],
-                1.0,
-                gains[:, g : g + 1, :].to_broadcast([P, width, PACK]),
-                ALU.min,
+            return hidden
+
+        def sign_weight(g, dealt):
+            signed = ring.tile([P, PASS, PACK], BF16, name="signed%d" % g, tag="signed", bufs=2, align_bytes=64)
+            nc.vector.tensor_tensor(
+                signed[:],
+                dealt[:].rearrange("p (c j) -> p c j", j=PACK),
+                signs[:, g : g + 1, :].to_broadcast([P, PASS, PACK]),
                 ALU.mult,
             )
-            return hidden
+            return signed[:].rearrange("p c j -> p (c j)")
 
         def quantize_hidden(g, cols, hidden):
             nc.vector.quantize_mx(
@@ -267,13 +290,13 @@ def tile_list_chess_feature_value_kernel(
         rect00 = rectify(0, 0, banks0[0], 0)
         dealt = round_weight(raw_wp[1, 0], "wp10", False, "B")
         raw_w2 = [load_weight(w2[g * PASS : (g + 1) * PASS, :], "raw_w2%d" % g, "IC"[g]) for g in range(2)]
-        h00 = finish_hidden(0, c0, rect00, "F")
         wp1 = [quantize_weight(dealt, "wp10", 1)]
         dealt = round_weight(raw_wp[1, 1], "wp11", False, "B")
-        quantize_hidden(0, c0, h00)
-        wp1.append(quantize_weight(dealt, "wp11", 1))
-        h01 = finish_hidden(0, c1, rect00, "G")
         rect01 = rectify(0, 1, banks0[1], 0)
+        wp1.append(quantize_weight(dealt, "wp11", 1))
+        h00 = finish_hidden(0, slice(0, 512), rect00, "F")
+        quantize_hidden(0, slice(0, 512), h00)
+        h01 = finish_hidden(0, slice(512, 1024), rect01, "G")
         banks1 = []
         for half in range(2):
             banks1.append(open_banks(1, half))
@@ -281,37 +304,35 @@ def tile_list_chess_feature_value_kernel(
                 for a in (THREAT, 0, 1):
                     first_pass(banks1[half][t], 1, t, half, a, None if a == THREAT else wp1[a], a == THREAT, a == 1)
         dealt0 = round_weight(raw_w2[0], "w20", False, "F")
-        quantize_hidden(0, c1, h01)
+        quantize_hidden(0, slice(512, 1024), h01)
+        signed0 = sign_weight(0, dealt0)
         dealt1 = round_weight(raw_w2[1], "w21", False, "G")
-        w2_mx = [quantize_weight(dealt0, "w20", 1)]
+        w2_mx = [quantize_weight(signed0, "w20", 1)]
+        signed1 = sign_weight(1, dealt1)
         rect10 = rectify(1, 0, banks1[0], 0)
+        w2_mx.append(quantize_weight(signed1, "w21", 1))
         h10 = finish_hidden(1, c0, rect10)
-        w2_mx.append(quantize_weight(dealt1, "w21", 1))
-        h11 = finish_hidden(1, c1, rect10)
         quantize_hidden(1, c0, h10)
-        y0 = second_stage(c0, w2_mx)
-        h02 = finish_hidden(0, c2, rect01)
+        h11 = finish_hidden(1, c1, rect10)
+        y0 = second_stage(c0, w2_mx, True)
         quantize_hidden(1, c1, h11)
-        y1 = second_stage(c1, w2_mx)
-        h03 = finish_hidden(0, late, rect01)
-        quantize_hidden(0, c2, h02)
-        r0 = round_y(c0, y0)
-        quantize_hidden(0, late, h03)
-        rect11 = rectify(1, 1, banks1[1], 0)
+        rect11 = rectify(1, 1, banks1[1], 2)
         h12 = finish_hidden(1, c2, rect11)
-        quantize_y(c0, r0)
-        h13 = finish_hidden(1, c3, rect11)
         quantize_hidden(1, c2, h12)
-        y2 = second_stage(c2, w2_mx)
-        h14 = finish_hidden(1, c4, rect11)
+        y1 = second_stage(c1, w2_mx, True)
+        h13 = finish_hidden(1, c3, rect11)
         quantize_hidden(1, c3, h13)
-        y3 = second_stage(c3, w2_mx)
-        r1 = round_y(c1, y1)
+        h14 = finish_hidden(1, c4, rect11)
         quantize_hidden(1, c4, h14)
+        r0 = round_y(c0, y0)
+        r1 = round_y(c1, y1)
+        quantize_y(c0, r0)
+        y2 = second_stage(c2, w2_mx)
+        y3 = second_stage(c3, w2_mx)
         y4 = second_stage(c4, w2_mx)
-        r2 = round_y(c2, y2)
         quantize_y(c1, r1)
         store_codes(slice(0, 512))
+        r2 = round_y(c2, y2)
         r3 = round_y(c3, y3)
         quantize_y(c2, r2)
         store_codes(c2)

@@ -101,6 +101,10 @@ def tile_list_chess_feature_value_kernel(
         nc.vector.tensor_tensor(inverse[:], inverse[:], rough[:], ALU.add)
         root = keep.tile([P, 2 * PACK], F32, name="root")
         nc.vector.tensor_scalar(root[:], inverse[:], 0.5, None, ALU.mult)
+        root_bias = keep.tile([P, 2 * PACK], F32, name="root_bias")
+        nc.vector.tensor_tensor(root_bias[:], root[:], bias[:].rearrange("p g t -> p (g t)"), ALU.mult)
+        ceiling = keep.tile([P, 2, PACK], BF16, name="ceiling")
+        nc.vector.tensor_copy(ceiling[:].rearrange("p g t -> p (g t)"), magnitude[:])
         positive = keep.tile([P, 2, PACK], F32, name="positive")
         nc.vector.tensor_scalar(positive[:], gains[:], 0.0, None, ALU.is_ge)
         signs = keep.tile([P, 2, PACK], BF16, name="signs")
@@ -164,17 +168,12 @@ def tile_list_chess_feature_value_kernel(
                 stop=stop,
             )
 
-        def rectify(g, half, banks, on_vector):
+        def rectify(g, half, banks):
             rectified = ring.tile([P, PACK, BANK], F32, name="rect%d%d" % (g, half), tag="rectified", bufs=3)
             for t in range(PACK):
-                if t < on_vector:
-                    nc.vector.tensor_scalar(rectified[:, t, :], banks[t][:], bias[:, g, t : t + 1], 0.0, ALU.add, ALU.max)
-                else:
-                    nc.scalar.activation(rectified[:, t, :], banks[t][:], ACT.Relu, bias=bias[:, g, t : t + 1])
-            for t in list(range(on_vector, PACK)) + list(range(on_vector)):
-                column = g * PACK + t
-                nc.vector.tensor_scalar(
-                    rectified[:, t, :], rectified[:, t, :], 1.0, root[:, column : column + 1], ALU.min, ALU.mult
+                column = slice(g * PACK + t, g * PACK + t + 1)
+                nc.scalar.activation(
+                    rectified[:, t, :], banks[t][:], ACT.Relu, bias=root_bias[:, column], scale=root[:, column]
                 )
             return rectified
 
@@ -195,6 +194,11 @@ def tile_list_chess_feature_value_kernel(
                 ACT.Square,
             )
             return hidden
+
+        def cap_hidden(g, hidden):
+            nc.vector.tensor_tensor(
+                hidden[:], hidden[:], ceiling[:, g : g + 1, :].to_broadcast(list(hidden.shape)), ALU.min
+            )
 
         def sign_weight(g, dealt):
             signed = ring.tile([P, PASS, PACK], BF16, name="signed%d" % g, tag="signed", bufs=2, align_bytes=64)
@@ -218,7 +222,7 @@ def tile_list_chess_feature_value_kernel(
         y_rows = out_0.rearrange("(p t) j -> p t j", t=PACK)
         y_words = out_1[0].rearrange("p m t -> p (m t)").bitcast(I32)
 
-        def second_stage(cols, w2_mx, last_on_vector=False):
+        def second_stage(cols, w2_mx, on_vector=0):
             width = cols.stop - cols.start
             side = BANK // width
             banks = [psum.tile([P, BANK], F32, name="ybank%d_%d" % (cols.start, b), tag="bank") for b in range(PACK // side)]
@@ -237,7 +241,7 @@ def tile_list_chess_feature_value_kernel(
             y = ring.tile([P, PACK, width], F32, name="y%d" % cols.start, tag="y", bufs=5)
             for b in range(PACK // side):
                 dst = y[:, b * side : (b + 1) * side, :].rearrange("p t n -> p (t n)")
-                if last_on_vector and b == len(banks) - 1:
+                if b >= len(banks) - on_vector:
                     nc.vector.tensor_copy(dst, banks[b][:])
                 else:
                     nc.scalar.copy(dst, banks[b][:])
@@ -287,15 +291,14 @@ def tile_list_chess_feature_value_kernel(
         chunks = [slice(0, 256), slice(256, 512), slice(512, 768), slice(768, 896), slice(896, 1024)]
         c0, c1, c2, c3, c4 = chunks
         late = slice(768, 1024)
-        rect00 = rectify(0, 0, banks0[0], 0)
+        rect00 = rectify(0, 0, banks0[0])
         dealt = round_weight(raw_wp[1, 0], "wp10", False, "B")
         raw_w2 = [load_weight(w2[g * PASS : (g + 1) * PASS, :], "raw_w2%d" % g, "IC"[g]) for g in range(2)]
         wp1 = [quantize_weight(dealt, "wp10", 1)]
         dealt = round_weight(raw_wp[1, 1], "wp11", False, "B")
-        rect01 = rectify(0, 1, banks0[1], 0)
         wp1.append(quantize_weight(dealt, "wp11", 1))
         h00 = finish_hidden(0, slice(0, 512), rect00, "F")
-        quantize_hidden(0, slice(0, 512), h00)
+        rect01 = rectify(0, 1, banks0[1])
         h01 = finish_hidden(0, slice(512, 1024), rect01, "G")
         banks1 = []
         for half in range(2):
@@ -303,26 +306,34 @@ def tile_list_chess_feature_value_kernel(
             for t in range(PACK):
                 for a in (THREAT, 0, 1):
                     first_pass(banks1[half][t], 1, t, half, a, None if a == THREAT else wp1[a], a == THREAT, a == 1)
-        dealt0 = round_weight(raw_w2[0], "w20", False, "F")
-        quantize_hidden(0, slice(512, 1024), h01)
+        dealt0 = round_weight(raw_w2[0], "w20", False, "J")
+        cap_hidden(0, h00)
         signed0 = sign_weight(0, dealt0)
-        dealt1 = round_weight(raw_w2[1], "w21", False, "G")
+        quantize_hidden(0, slice(0, 512), h00)
+        dealt1 = round_weight(raw_w2[1], "w21", False, "K")
         w2_mx = [quantize_weight(signed0, "w20", 1)]
         signed1 = sign_weight(1, dealt1)
-        rect10 = rectify(1, 0, banks1[0], 0)
-        w2_mx.append(quantize_weight(signed1, "w21", 1))
+        rect10 = rectify(1, 0, banks1[0])
         h10 = finish_hidden(1, c0, rect10)
-        quantize_hidden(1, c0, h10)
         h11 = finish_hidden(1, c1, rect10)
-        y0 = second_stage(c0, w2_mx, True)
+        cap_hidden(1, h10)
+        w2_mx.append(quantize_weight(signed1, "w21", 1))
+        quantize_hidden(1, c0, h10)
+        cap_hidden(1, h11)
+        cap_hidden(0, h01)
         quantize_hidden(1, c1, h11)
-        rect11 = rectify(1, 1, banks1[1], 2)
+        quantize_hidden(0, slice(512, 1024), h01)
+        rect11 = rectify(1, 1, banks1[1])
+        y0 = second_stage(c0, w2_mx, 2)
         h12 = finish_hidden(1, c2, rect11)
+        cap_hidden(1, h12)
         quantize_hidden(1, c2, h12)
-        y1 = second_stage(c1, w2_mx, True)
+        y1 = second_stage(c1, w2_mx, 1)
         h13 = finish_hidden(1, c3, rect11)
+        cap_hidden(1, h13)
         quantize_hidden(1, c3, h13)
         h14 = finish_hidden(1, c4, rect11)
+        cap_hidden(1, h14)
         quantize_hidden(1, c4, h14)
         r0 = round_y(c0, y0)
         r1 = round_y(c1, y1)

@@ -35,9 +35,6 @@ def tile_list_chess_feature_value_kernel(
         ring = ctx.enter_context(tc.tile_pool(name="ring", bufs=1))
         psum = ctx.enter_context(tc.psum_pool(name="psum", bufs=8))
 
-        offsets = keep.tile([P, S // 16], U16, name="offsets")
-        nc.sync.dma_start(offsets[:], offs)
-
         def slot(shape, dtype, name, tag):
             return ring.tile(shape, dtype, name=name, tag=tag, bufs=1, align_bytes=64)
 
@@ -54,41 +51,43 @@ def tile_list_chess_feature_value_kernel(
         def load_wp(g, a, tag):
             return load_weight(wp[a * PASS : (a + 1) * PASS, g * PASS : (g + 1) * PASS], "raw_wp%d%d" % (g, a), tag)
 
-        def pick(a, words, parts=1):
-            picked[a] = keep.tile([P, S], U32, name="picked%d" % a, align_bytes=64)
+        def pick(a, words, tag, parts=1):
+            picked[a] = slot([P, S], U32, "picked%d" % a, tag)
             width = S // parts
             for c0 in range(0, S, width):
                 nc.vector.tensor_copy(
                     picked[a][:, c0 : c0 + width], words[:].indirect(offsets[:, c0 // 16 : (c0 + width) // 16])
                 )
 
-        wt_raw = [slot([P, 2 * PASS], U8, "wt_raw%d" % g, "CE"[g]) for g in range(2)]
-        for g in range(2):
-            nc.sync.dma_start(wt_raw[g][:].bitcast(I32), wt_words[0, :, 2 * g * PASS : 2 * (g + 1) * PASS].bitcast(I32))
+        table_0 = load_table(0, "A")
+        offsets = keep.tile([P, S // 16], U16, name="offsets")
+        nc.sync.dma_start(offsets[:], offs)
+        wt_raw = keep.tile([P, 2 * H], U8, name="wt_raw", align_bytes=64)
+        nc.sync.dma_start(wt_raw[:].bitcast(I32), wt_words[0].bitcast(I32))
         bias = keep.tile([P, 2, PACK], F32, name="bias")
         nc.sync.dma_start(bias[:], bh.rearrange("(g p t) -> p g t", g=2, t=PACK))
         gains = keep.tile([P, 2, PACK], F32, name="gains")
         nc.sync.dma_start(gains[:], gain.rearrange("(g p t) -> p g t", g=2, t=PACK))
-        table_0 = load_table(0, "A")
         raw_wp = {}
-        raw_wp[0, 0] = load_wp(0, 0, "B")
+        raw_wp[0, 0] = load_wp(0, 0, "L")
+        table_threat = load_table(THREAT, "C")
+        raw_wp[0, 1] = load_wp(0, 1, "E")
+        table_1 = load_table(1, "B")
+        raw_wp[1, 0] = load_wp(1, 0, "M")
+        raw_wp[1, 1] = load_wp(1, 1, "N")
 
         table_scales = slot([P, T], U8, "table_scales", "D")
         nc.vector.memset(table_scales[:].bitcast(I32), 0)
-        wt_scales_raw = keep.tile([P, H], U8, name="wt_scales_raw", align_bytes=64)
+        wt_scales_raw = slot([P, H], U8, "wt_scales_raw", "W")
         nc.vector.memset(wt_scales_raw[:].bitcast(I32), 0)
         for q in range(4):
-            (nc.gpsimd if q < 3 else nc.sync).dma_start(
+            nc.gpsimd.dma_start(
                 table_scales[32 * q + 4 : 32 * q + 12, :].bitcast(I32), tab_scales[0:2, 4 * q : 4 * q + 4, :].bitcast(I32)
             )
-        for q in range(4):
-            nc.sync.dma_start(
-                table_scales[32 * q : 32 * q + 4, :].bitcast(I32), tab_scales[THREAT, 4 * q : 4 * q + 4, :].bitcast(I32)
-            )
-        for q in range(4):
-            (nc.sync if q < 1 else nc.gpsimd).dma_start(
-                wt_scales_raw[32 * q : 32 * q + 4, :].bitcast(I32), wt_scales[0, 4 * q : 4 * q + 4, :].bitcast(I32)
-            )
+        for r in range(4):
+            nc.gpsimd.dma_start(table_scales[r:P:32, :].bitcast(I32), tab_scales[THREAT, r:16:4, :].bitcast(I32))
+        for r in range(4):
+            nc.gpsimd.dma_start(wt_scales_raw[r:P:32, :].bitcast(I32), wt_scales[0, r:16:4, :].bitcast(I32))
 
         magnitude = keep.tile([P, 2 * PACK], F32, name="magnitude")
         nc.scalar.activation(magnitude[:], gains[:].rearrange("p g t -> p (g t)"), ACT.Abs)
@@ -115,13 +114,11 @@ def tile_list_chess_feature_value_kernel(
         for g in range(2):
             nc.vector.tensor_copy(
                 wt_dealt[:, 2 * g * PASS : 2 * (g + 1) * PASS].rearrange("p (t m b) -> p m t b", t=PACK, b=2),
-                wt_raw[g][:].rearrange("p (m t b) -> p m t b", t=PACK, b=2),
+                wt_raw[:, 2 * g * PASS : 2 * (g + 1) * PASS].rearrange("p (m t b) -> p m t b", t=PACK, b=2),
             )
-        table_threat = load_table(THREAT, "C")
-        raw_wp[0, 1] = load_wp(0, 1, "E")
 
         picked = {}
-        pick(0, table_0)
+        pick(0, table_0, "O")
         picked_scales = keep.tile([P, S], U8, name="picked_scales", align_bytes=64)
         nc.vector.tensor_copy(picked_scales[:], table_scales[:].indirect(offsets[:]))
 
@@ -135,9 +132,10 @@ def tile_list_chess_feature_value_kernel(
                 nc.vector.tensor_copy(dst, src)
             return dealt
 
-        def quantize_weight(dealt, name, parts):
-            codes = keep.tile([P, PASS], U32, name=name + "_codes", align_bytes=64)
-            plane = keep.tile([P, PASS], U8, name=name + "_plane", align_bytes=64)
+        def quantize_weight(dealt, name, parts, tags=None):
+            tags = tags or (name + "_codes", name + "_plane")
+            codes = slot([P, PASS], U32, name + "_codes", tags[0])
+            plane = slot([P, PASS], U8, name + "_plane", tags[1])
             width = PASS // parts
             for part in range(parts):
                 cols = slice(part * width, (part + 1) * width)
@@ -269,11 +267,10 @@ def tile_list_chess_feature_value_kernel(
 
         banks0 = [open_banks(0, half) for half in range(2)]
         weights = quantize_weight(round_weight(raw_wp[0, 0], "wp00", True, "H"), "wp00", 1)
-        table_1 = load_table(1, "B")
         for half in range(2):
             for t in range(PACK):
                 first_pass(banks0[half][t], 0, t, half, 0, weights, True, False)
-        pick(THREAT, table_threat)
+        pick(THREAT, table_threat, "D")
         nc.vector.tensor_copy(
             wt_plane[:].rearrange("p (g t m) -> p g m t", g=2, t=PACK),
             wt_scales_raw[:].rearrange("p (g m t) -> p g m t", g=2, t=PACK),
@@ -281,10 +278,8 @@ def tile_list_chess_feature_value_kernel(
         for half in range(2):
             for t in range(PACK):
                 first_pass(banks0[half][t], 0, t, half, THREAT, None, False, False)
-        raw_wp[1, 0] = load_wp(1, 0, "C")
-        weights = quantize_weight(round_weight(raw_wp[0, 1], "wp01", True, "I"), "wp01", 1)
-        raw_wp[1, 1] = load_wp(1, 1, "E")
-        pick(1, table_1, 2)
+        weights = quantize_weight(round_weight(raw_wp[0, 1], "wp01", True, "I"), "wp01", 1, ("C", "W"))
+        pick(1, table_1, "I", 2)
         for half in range(2):
             for t in range(PACK):
                 first_pass(banks0[half][t], 0, t, half, 1, weights, False, True)
@@ -293,7 +288,7 @@ def tile_list_chess_feature_value_kernel(
         late = slice(768, 1024)
         rect00 = rectify(0, 0, banks0[0])
         dealt = round_weight(raw_wp[1, 0], "wp10", False, "B")
-        raw_w2 = [load_weight(w2[g * PASS : (g + 1) * PASS, :], "raw_w2%d" % g, "IC"[g]) for g in range(2)]
+        raw_w2 = [load_weight(w2[g * PASS : (g + 1) * PASS, :], "raw_w2%d" % g, "AL"[g]) for g in range(2)]
         wp1 = [quantize_weight(dealt, "wp10", 1)]
         dealt = round_weight(raw_wp[1, 1], "wp11", False, "B")
         wp1.append(quantize_weight(dealt, "wp11", 1))

@@ -23,7 +23,17 @@ BANK = 512
 CHUNK = 256
 THREAT = 2
 SCALE_ROW = {THREAT: 0, 0: 4, 1: 8}
-VECTOR_M = 84
+KIB = 1024
+AT_WP00_CODES = 0
+AT_SCALES = 1 * KIB
+AT_PICKED_THREAT = 2 * KIB
+AT_WP11 = 8 * KIB
+AT_THREAT = 16 * KIB - 64
+AT_WP10 = 16 * KIB
+AT_WP01_CODES = 24 * KIB
+AT_W20 = 26 * KIB
+AT_TABLE1 = 34 * KIB
+AT_W21 = 38 * KIB
 
 
 def tile_list_chess_feature_value_kernel(
@@ -33,9 +43,12 @@ def tile_list_chess_feature_value_kernel(
     with ExitStack() as ctx:
         keep = ctx.enter_context(tc.tile_pool(name="keep", bufs=1))
         ring = ctx.enter_context(tc.tile_pool(name="ring", bufs=1))
+        lap = ctx.enter_context(tc.tile_pool(name="lap", bufs=1))
         psum = ctx.enter_context(tc.psum_pool(name="psum", bufs=8))
 
         def slot(shape, dtype, name, tag):
+            if isinstance(tag, int):
+                return lap.tile(shape, dtype, name=name, offset=tag, align_bytes=64)
             return ring.tile(shape, dtype, name=name, tag=tag, bufs=1, align_bytes=64)
 
         def load_table(a, tag):
@@ -70,13 +83,11 @@ def tile_list_chess_feature_value_kernel(
         nc.sync.dma_start(gains[:], gain.rearrange("(g p t) -> p g t", g=2, t=PACK))
         raw_wp = {}
         raw_wp[0, 0] = load_wp(0, 0, "L")
-        table_threat = load_table(THREAT, "C")
+        table_threat = load_table(THREAT, AT_THREAT)
         raw_wp[0, 1] = load_wp(0, 1, "E")
-        table_1 = load_table(1, "B")
-        raw_wp[1, 0] = load_wp(1, 0, "M")
-        raw_wp[1, 1] = load_wp(1, 1, "N")
+        table_1 = load_table(1, AT_TABLE1)
 
-        table_scales = slot([P, T], U8, "table_scales", "D")
+        table_scales = slot([P, T], U8, "table_scales", AT_SCALES)
         nc.vector.memset(table_scales[:].bitcast(I32), 0)
         wt_scales_raw = slot([P, H], U8, "wt_scales_raw", "W")
         nc.vector.memset(wt_scales_raw[:].bitcast(I32), 0)
@@ -266,11 +277,14 @@ def tile_list_chess_feature_value_kernel(
             return [psum.tile([P, BANK], F32, name="bank%d%d%d" % (g, half, t), tag="bank") for t in range(PACK)]
 
         banks0 = [open_banks(0, half) for half in range(2)]
-        weights = quantize_weight(round_weight(raw_wp[0, 0], "wp00", True, "H"), "wp00", 1)
+        weights = quantize_weight(round_weight(raw_wp[0, 0], "wp00", True, "H"), "wp00", 1, (AT_WP00_CODES, "wp00_plane"))
         for half in range(2):
             for t in range(PACK):
                 first_pass(banks0[half][t], 0, t, half, 0, weights, True, False)
-        pick(THREAT, table_threat, "D")
+        pick(THREAT, table_threat, AT_PICKED_THREAT)
+        raw_wp[1, 0] = load_wp(1, 0, AT_WP10)
+        raw_wp[1, 1] = load_wp(1, 1, AT_WP11)
+        raw_w2 = [load_weight(w2[0:PASS, :], "raw_w20", AT_W20)]
         nc.vector.tensor_copy(
             wt_plane[:].rearrange("p (g t m) -> p g m t", g=2, t=PACK),
             wt_scales_raw[:].rearrange("p (g m t) -> p g m t", g=2, t=PACK),
@@ -278,8 +292,9 @@ def tile_list_chess_feature_value_kernel(
         for half in range(2):
             for t in range(PACK):
                 first_pass(banks0[half][t], 0, t, half, THREAT, None, False, False)
-        weights = quantize_weight(round_weight(raw_wp[0, 1], "wp01", True, "I"), "wp01", 1, ("C", "W"))
+        weights = quantize_weight(round_weight(raw_wp[0, 1], "wp01", True, "I"), "wp01", 1, (AT_WP01_CODES, "W"))
         pick(1, table_1, "I", 2)
+        raw_w2.append(load_weight(w2[PASS : 2 * PASS, :], "raw_w21", AT_W21))
         for half in range(2):
             for t in range(PACK):
                 first_pass(banks0[half][t], 0, t, half, 1, weights, False, True)
@@ -287,10 +302,9 @@ def tile_list_chess_feature_value_kernel(
         c0, c1, c2, c3, c4 = chunks
         late = slice(768, 1024)
         rect00 = rectify(0, 0, banks0[0])
-        dealt = round_weight(raw_wp[1, 0], "wp10", False, "B")
-        raw_w2 = [load_weight(w2[g * PASS : (g + 1) * PASS, :], "raw_w2%d" % g, "AL"[g]) for g in range(2)]
+        dealt = round_weight(raw_wp[1, 0], "wp10", False, AT_TABLE1)
         wp1 = [quantize_weight(dealt, "wp10", 1)]
-        dealt = round_weight(raw_wp[1, 1], "wp11", False, "B")
+        dealt = round_weight(raw_wp[1, 1], "wp11", False, AT_WP10)
         wp1.append(quantize_weight(dealt, "wp11", 1))
         h00 = finish_hidden(0, slice(0, 512), rect00, "F")
         rect01 = rectify(0, 1, banks0[1])
@@ -301,11 +315,11 @@ def tile_list_chess_feature_value_kernel(
             for t in range(PACK):
                 for a in (THREAT, 0, 1):
                     first_pass(banks1[half][t], 1, t, half, a, None if a == THREAT else wp1[a], a == THREAT, a == 1)
-        dealt0 = round_weight(raw_w2[0], "w20", False, "J")
+        dealt0 = round_weight(raw_w2[0], "w20", False, AT_WP11)
         cap_hidden(0, h00)
         signed0 = sign_weight(0, dealt0)
         quantize_hidden(0, slice(0, 512), h00)
-        dealt1 = round_weight(raw_w2[1], "w21", False, "K")
+        dealt1 = round_weight(raw_w2[1], "w21", False, AT_W20)
         w2_mx = [quantize_weight(signed0, "w20", 1)]
         signed1 = sign_weight(1, dealt1)
         rect10 = rectify(1, 0, banks1[0])

@@ -24,16 +24,15 @@ CHUNK = 256
 THREAT = 2
 SCALE_ROW = {THREAT: 0, 0: 4, 1: 8}
 KIB = 1024
-AT_WP00_CODES = 0
-AT_SCALES = 1 * KIB
-AT_PICKED_THREAT = 2 * KIB
-AT_WP11 = 8 * KIB
-AT_THREAT = 16 * KIB - 64
-AT_WP10 = 16 * KIB
-AT_WP01_CODES = 24 * KIB
-AT_W20 = 26 * KIB
+AT_THREAT = 0
+AT_WP11 = 0
+AT_W20 = 8 * KIB
+AT_WT = 16 * KIB - 64
+AT_WP01 = 18 * KIB - 128
+AT_WP10 = 26 * KIB
+AT_TABLE0 = 34 * KIB - 64
 AT_TABLE1 = 34 * KIB
-AT_W21 = 38 * KIB
+AT_SCALES = 50 * KIB
 
 
 def tile_list_chess_feature_value_kernel(
@@ -72,31 +71,29 @@ def tile_list_chess_feature_value_kernel(
                     picked[a][:, c0 : c0 + width], words[:].indirect(offsets[:, c0 // 16 : (c0 + width) // 16])
                 )
 
-        table_0 = load_table(0, "A")
+        wt_raw = slot([P, 2 * H], U8, "wt_raw", AT_WT)
+        nc.sync.dma_start(wt_raw[:].bitcast(I32), wt_words[0].bitcast(I32))
         offsets = keep.tile([P, S // 16], U16, name="offsets")
         nc.sync.dma_start(offsets[:], offs)
-        wt_raw = keep.tile([P, 2 * H], U8, name="wt_raw", align_bytes=64)
-        nc.sync.dma_start(wt_raw[:].bitcast(I32), wt_words[0].bitcast(I32))
+        table_0 = load_table(0, AT_TABLE0)
         bias = keep.tile([P, 2, PACK], F32, name="bias")
         nc.sync.dma_start(bias[:], bh.rearrange("(g p t) -> p g t", g=2, t=PACK))
         gains = keep.tile([P, 2, PACK], F32, name="gains")
         nc.sync.dma_start(gains[:], gain.rearrange("(g p t) -> p g t", g=2, t=PACK))
         raw_wp = {}
         raw_wp[0, 0] = load_wp(0, 0, "L")
-        table_threat = load_table(THREAT, AT_THREAT)
-        raw_wp[0, 1] = load_wp(0, 1, "E")
-        table_1 = load_table(1, AT_TABLE1)
 
         table_scales = slot([P, T], U8, "table_scales", AT_SCALES)
         nc.vector.memset(table_scales[:].bitcast(I32), 0)
         wt_scales_raw = slot([P, H], U8, "wt_scales_raw", "W")
         nc.vector.memset(wt_scales_raw[:].bitcast(I32), 0)
-        for q in range(4):
-            nc.gpsimd.dma_start(
-                table_scales[32 * q + 4 : 32 * q + 12, :].bitcast(I32), tab_scales[0:2, 4 * q : 4 * q + 4, :].bitcast(I32)
-            )
-        for r in range(4):
-            nc.gpsimd.dma_start(table_scales[r:P:32, :].bitcast(I32), tab_scales[THREAT, r:16:4, :].bitcast(I32))
+        picked_plane = [keep.tile([P, S], U8, name="picked_plane%d" % a, align_bytes=64) for a in range(3)]
+        for a in range(3):
+            nc.vector.memset(picked_plane[a][:].bitcast(I32), 0)
+        nc.scalar.dma_start(
+            table_scales[0:P:4, :].bitcast(I32), tab_scales[0:2].rearrange("a q t -> (a q) t").bitcast(I32)
+        )
+        nc.scalar.dma_start(table_scales[2:P:8, :].bitcast(I32), tab_scales[THREAT].bitcast(I32))
         for r in range(4):
             nc.gpsimd.dma_start(wt_scales_raw[r:P:32, :].bitcast(I32), wt_scales[0, r:16:4, :].bitcast(I32))
 
@@ -128,10 +125,22 @@ def tile_list_chess_feature_value_kernel(
                 wt_raw[:, 2 * g * PASS : 2 * (g + 1) * PASS].rearrange("p (m t b) -> p m t b", t=PACK, b=2),
             )
 
-        picked = {}
-        pick(0, table_0, "O")
+        table_threat = load_table(THREAT, AT_THREAT)
+        raw_wp[0, 1] = load_wp(0, 1, AT_WP01)
+
         picked_scales = keep.tile([P, S], U8, name="picked_scales", align_bytes=64)
         nc.vector.tensor_copy(picked_scales[:], table_scales[:].indirect(offsets[:]))
+        for a, queue in ((0, nc.gpsimd), (THREAT, nc.gpsimd), (1, nc.scalar)):
+            for r in range(4):
+                rows = slice(2 + 8 * r, P, 32) if a == THREAT else slice(64 * a + 4 * r, 64 * (a + 1), 16)
+                queue.dma_start(
+                    picked_plane[a][SCALE_ROW[a] + r : P : 32, :].bitcast(I32),
+                    picked_scales[rows, :].bitcast(I32),
+                )
+        picked = {}
+        pick(0, table_0, AT_SCALES)
+        table_1 = load_table(1, AT_TABLE1)
+        raw_wp[1, 0] = load_wp(1, 0, AT_WP10)
 
         def round_weight(raw, name, shared, tag):
             dealt = slot([P, PACK * PASS], BF16, name, tag)
@@ -172,7 +181,7 @@ def tile_list_chess_feature_value_kernel(
                 lhsT=lhs,
                 lhsT_scale=lhs_scale,
                 rhs=picked[a][:, cols].bitcast(E4M3),
-                rhs_scale=picked_scales[SCALE_ROW[a] :, cols],
+                rhs_scale=picked_plane[a][SCALE_ROW[a] :, cols],
                 start=start,
                 stop=stop,
             )
@@ -277,12 +286,11 @@ def tile_list_chess_feature_value_kernel(
             return [psum.tile([P, BANK], F32, name="bank%d%d%d" % (g, half, t), tag="bank") for t in range(PACK)]
 
         banks0 = [open_banks(0, half) for half in range(2)]
-        weights = quantize_weight(round_weight(raw_wp[0, 0], "wp00", True, "H"), "wp00", 1, (AT_WP00_CODES, "wp00_plane"))
+        weights = quantize_weight(round_weight(raw_wp[0, 0], "wp00", True, "H"), "wp00", 1)
         for half in range(2):
             for t in range(PACK):
                 first_pass(banks0[half][t], 0, t, half, 0, weights, True, False)
-        pick(THREAT, table_threat, AT_PICKED_THREAT)
-        raw_wp[1, 0] = load_wp(1, 0, AT_WP10)
+        pick(THREAT, table_threat, "D")
         raw_wp[1, 1] = load_wp(1, 1, AT_WP11)
         raw_w2 = [load_weight(w2[0:PASS, :], "raw_w20", AT_W20)]
         nc.vector.tensor_copy(
@@ -292,9 +300,9 @@ def tile_list_chess_feature_value_kernel(
         for half in range(2):
             for t in range(PACK):
                 first_pass(banks0[half][t], 0, t, half, THREAT, None, False, False)
-        weights = quantize_weight(round_weight(raw_wp[0, 1], "wp01", True, "I"), "wp01", 1, (AT_WP01_CODES, "W"))
+        weights = quantize_weight(round_weight(raw_wp[0, 1], "wp01", True, "I"), "wp01", 1, ("wp01_codes", "W"))
+        raw_w2.append(load_weight(w2[PASS : 2 * PASS, :], "raw_w21", AT_WP01))
         pick(1, table_1, "I", 2)
-        raw_w2.append(load_weight(w2[PASS : 2 * PASS, :], "raw_w21", AT_W21))
         for half in range(2):
             for t in range(PACK):
                 first_pass(banks0[half][t], 0, t, half, 1, weights, False, True)

@@ -33,6 +33,7 @@ AT_WP10 = 26 * KIB
 AT_TABLE0 = 34 * KIB - 64
 AT_TABLE1 = 34 * KIB
 AT_SCALES = 50 * KIB
+AT_PICKED0 = 50 * KIB + 64
 
 
 def tile_list_chess_feature_value_kernel(
@@ -112,10 +113,6 @@ def tile_list_chess_feature_value_kernel(
         nc.vector.tensor_tensor(root_bias[:], root[:], bias[:].rearrange("p g t -> p (g t)"), ALU.mult)
         ceiling = keep.tile([P, 2, PACK], BF16, name="ceiling")
         nc.vector.tensor_copy(ceiling[:].rearrange("p g t -> p (g t)"), magnitude[:])
-        positive = keep.tile([P, 2, PACK], F32, name="positive")
-        nc.vector.tensor_scalar(positive[:], gains[:], 0.0, None, ALU.is_ge)
-        signs = keep.tile([P, 2, PACK], BF16, name="signs")
-        nc.vector.tensor_scalar(signs[:], positive[:], 2.0, -1.0, ALU.mult, ALU.add)
 
         wt_dealt = keep.tile([P, 2 * H], U8, name="wt_dealt", align_bytes=64)
         wt_plane = keep.tile([P, H], U8, name="wt_plane", align_bytes=64)
@@ -138,8 +135,13 @@ def tile_list_chess_feature_value_kernel(
                     picked_scales[rows, :].bitcast(I32),
                 )
         picked = {}
-        pick(0, table_0, AT_SCALES)
+        pick(0, table_0, AT_PICKED0)
         table_1 = load_table(1, AT_TABLE1)
+        positive = slot([P, 2, PACK], F32, "positive", AT_SCALES)
+        nc.vector.tensor_scalar(positive[:], gains[:], 0.0, None, ALU.is_ge)
+        signs = keep.tile([P, 2, PACK], BF16, name="signs")
+        nc.vector.tensor_scalar(signs[:], positive[:], 2.0, -1.0, ALU.mult, ALU.add)
+
         raw_wp[1, 0] = load_wp(1, 0, AT_WP10)
 
         def round_weight(raw, name, shared, tag):
@@ -266,12 +268,10 @@ def tile_list_chess_feature_value_kernel(
             nc.sync.dma_start(y_rows[:, :, cols], y[:])
             return y
 
-        def round_y(cols, y):
+        def round_y(cols, y, copy=nc.vector.tensor_copy):
             width = cols.stop - cols.start
             rounded = ring.tile([P, width, PACK], BF16, name="yb%d" % cols.start, tag="rounded", bufs=3, align_bytes=64)
-            nc.vector.tensor_copy(
-                rounded[:].rearrange("p (c i) t -> p c t i", i=4), y[:].rearrange("p t (c i) -> p c t i", i=4)
-            )
+            copy(rounded[:].rearrange("p (c i) t -> p c t i", i=4), y[:].rearrange("p t (c i) -> p c t i", i=4))
             return rounded
 
         def quantize_y(cols, rounded):
@@ -345,7 +345,7 @@ def tile_list_chess_feature_value_kernel(
         h12 = finish_hidden(1, c2, rect11)
         cap_hidden(1, h12)
         quantize_hidden(1, c2, h12)
-        y1 = second_stage(c1, w2_mx, 1)
+        y1 = second_stage(c1, w2_mx)
         h13 = finish_hidden(1, c3, rect11)
         cap_hidden(1, h13)
         quantize_hidden(1, c3, h13)
@@ -364,7 +364,7 @@ def tile_list_chess_feature_value_kernel(
         r3 = round_y(c3, y3)
         quantize_y(c2, r2)
         store_codes(c2)
-        r4 = round_y(c4, y4)
+        r4 = round_y(c4, y4, nc.scalar.copy)
         quantize_y(c3, r3)
         quantize_y(c4, r4)
         store_codes(late)

@@ -127,7 +127,7 @@ def tile_list_chess_feature_value_kernel(
 
         picked_scales = keep.tile([P, S], U8, name="picked_scales", align_bytes=64)
         nc.vector.tensor_copy(picked_scales[:], table_scales[:].indirect(offsets[:]))
-        for a, queue in ((0, nc.gpsimd), (THREAT, nc.gpsimd), (1, nc.scalar)):
+        for a, queue in ((0, nc.gpsimd), (THREAT, nc.scalar), (1, nc.gpsimd)):
             for r in range(4):
                 rows = slice(2 + 8 * r, P, 32) if a == THREAT else slice(64 * a + 4 * r, 64 * (a + 1), 16)
                 queue.dma_start(

@@ -33,7 +33,8 @@ AT_WP10 = 26 * KIB
 AT_TABLE0 = 34 * KIB - 64
 AT_TABLE1 = 34 * KIB
 AT_SCALES = 50 * KIB
-AT_PICKED0 = 50 * KIB + 64
+AT_MAGNITUDE = 50 * KIB + 64
+AT_PICKED0 = 50 * KIB + 128
 
 
 def tile_list_chess_feature_value_kernel(
@@ -77,10 +78,6 @@ def tile_list_chess_feature_value_kernel(
         offsets = keep.tile([P, S // 16], U16, name="offsets")
         nc.sync.dma_start(offsets[:], offs)
         table_0 = load_table(0, AT_TABLE0)
-        bias = keep.tile([P, 2, PACK], F32, name="bias")
-        nc.sync.dma_start(bias[:], bh.rearrange("(g p t) -> p g t", g=2, t=PACK))
-        gains = keep.tile([P, 2, PACK], F32, name="gains")
-        nc.sync.dma_start(gains[:], gain.rearrange("(g p t) -> p g t", g=2, t=PACK))
         raw_wp = {}
         raw_wp[0, 0] = load_wp(0, 0, "L")
 
@@ -98,21 +95,12 @@ def tile_list_chess_feature_value_kernel(
         for r in range(4):
             nc.gpsimd.dma_start(wt_scales_raw[r:P:32, :].bitcast(I32), wt_scales[0, r:16:4, :].bitcast(I32))
 
-        magnitude = keep.tile([P, 2 * PACK], F32, name="magnitude")
-        nc.scalar.activation(magnitude[:], gains[:].rearrange("p g t -> p (g t)"), ACT.Abs)
-        rough = keep.tile([P, 2 * PACK], F32, name="rough")
-        nc.scalar.activation(rough[:], magnitude[:], ACT.Sqrt)
-        inverse = keep.tile([P, 2 * PACK], F32, name="inverse")
-        nc.vector.tensor_scalar(inverse[:], rough[:], 1e-30, None, ALU.max)
-        nc.vector.reciprocal(inverse[:], inverse[:])
-        nc.vector.tensor_tensor(inverse[:], inverse[:], magnitude[:], ALU.mult)
-        nc.vector.tensor_tensor(inverse[:], inverse[:], rough[:], ALU.add)
-        root = keep.tile([P, 2 * PACK], F32, name="root")
-        nc.vector.tensor_scalar(root[:], inverse[:], 0.5, None, ALU.mult)
-        root_bias = keep.tile([P, 2 * PACK], F32, name="root_bias")
-        nc.vector.tensor_tensor(root_bias[:], root[:], bias[:].rearrange("p g t -> p (g t)"), ALU.mult)
-        ceiling = keep.tile([P, 2, PACK], BF16, name="ceiling")
-        nc.vector.tensor_copy(ceiling[:].rearrange("p g t -> p (g t)"), magnitude[:])
+        gains_padded = keep.tile([P, 2, 2 * PACK], F32, name="gains_padded")
+        gains = gains_padded[:, :, 0:PACK]
+        nc.gpsimd.dma_start(gains, gain.rearrange("(g p t) -> p g t", g=2, t=PACK))
+        bias_padded = keep.tile([P, 2, 2 * PACK], F32, name="bias_padded")
+        bias = bias_padded[:, :, 0:PACK]
+        nc.gpsimd.dma_start(bias, bh.rearrange("(g p t) -> p g t", g=2, t=PACK))
 
         wt_dealt = keep.tile([P, 2 * H], U8, name="wt_dealt", align_bytes=64)
         wt_plane = keep.tile([P, H], U8, name="wt_plane", align_bytes=64)
@@ -127,6 +115,10 @@ def tile_list_chess_feature_value_kernel(
 
         picked_scales = keep.tile([P, S], U8, name="picked_scales", align_bytes=64)
         nc.vector.tensor_copy(picked_scales[:], table_scales[:].indirect(offsets[:]))
+        magnitude = slot([P, 2 * PACK], F32, "magnitude", AT_MAGNITUDE)
+        nc.scalar.activation(magnitude[:].rearrange("p (g t) -> p g t", g=2), gains, ACT.Abs)
+        rough = keep.tile([P, 2 * PACK], F32, name="rough")
+        nc.scalar.activation(rough[:], magnitude[:], ACT.Sqrt)
         for a, queue in ((0, nc.gpsimd), (THREAT, nc.scalar), (1, nc.gpsimd)):
             for r in range(4):
                 rows = slice(2 + 8 * r, P, 32) if a == THREAT else slice(64 * a + 4 * r, 64 * (a + 1), 16)
@@ -137,8 +129,21 @@ def tile_list_chess_feature_value_kernel(
         picked = {}
         pick(0, table_0, AT_PICKED0)
         table_1 = load_table(1, AT_TABLE1)
+        inverse = keep.tile([P, 2 * PACK], F32, name="inverse")
+        nc.vector.tensor_scalar(inverse[:], rough[:], 1e-30, None, ALU.max)
+        nc.vector.reciprocal(inverse[:], inverse[:])
+        nc.vector.tensor_tensor(inverse[:], inverse[:], magnitude[:], ALU.mult)
+        nc.vector.tensor_tensor(inverse[:], inverse[:], rough[:], ALU.add)
+        root = keep.tile([P, 2 * PACK], F32, name="root")
+        nc.vector.tensor_scalar(root[:], inverse[:], 0.5, None, ALU.mult)
+        root_bias = keep.tile([P, 2 * PACK], F32, name="root_bias")
+        nc.vector.tensor_tensor(
+            root_bias[:].rearrange("p (g t) -> p g t", g=2), root[:].rearrange("p (g t) -> p g t", g=2), bias, ALU.mult
+        )
+        ceiling = keep.tile([P, 2, PACK], BF16, name="ceiling")
+        nc.vector.tensor_copy(ceiling[:].rearrange("p g t -> p (g t)"), magnitude[:])
         positive = slot([P, 2, PACK], F32, "positive", AT_SCALES)
-        nc.vector.tensor_scalar(positive[:], gains[:], 0.0, None, ALU.is_ge)
+        nc.vector.tensor_scalar(positive[:], gains, 0.0, None, ALU.is_ge)
         signs = keep.tile([P, 2, PACK], BF16, name="signs")
         nc.vector.tensor_scalar(signs[:], positive[:], 2.0, -1.0, ALU.mult, ALU.add)
 
@@ -242,7 +247,7 @@ def tile_list_chess_feature_value_kernel(
         y_rows = out_0.rearrange("(p t) j -> p t j", t=PACK)
         y_words = out_1[0].rearrange("p m t -> p (m t)").bitcast(I32)
 
-        def second_stage(cols, w2_mx, on_vector=0):
+        def second_stage(cols, w2_mx, on_vector=0, into=None):
             width = cols.stop - cols.start
             side = BANK // width
             banks = [psum.tile([P, BANK], F32, name="ybank%d_%d" % (cols.start, b), tag="bank") for b in range(PACK // side)]
@@ -258,7 +263,10 @@ def tile_list_chess_feature_value_kernel(
                         start=(g == 0 and t % side == 0),
                         stop=(g == 1 and t % side == side - 1),
                     )
-            y = ring.tile([P, PACK, width], F32, name="y%d" % cols.start, tag="y", bufs=5)
+            if into is not None:
+                nc.scalar.copy(into, banks[0][:].rearrange("p (t n) -> p t n", t=PACK))
+                return into
+            y = ring.tile([P, PACK, width], F32, name="y%d" % cols.start, tag="y", bufs=4)
             for b in range(PACK // side):
                 dst = y[:, b * side : (b + 1) * side, :].rearrange("p t n -> p (t n)")
                 if b >= len(banks) - on_vector:
@@ -266,12 +274,12 @@ def tile_list_chess_feature_value_kernel(
                 else:
                     nc.scalar.copy(dst, banks[b][:])
             nc.sync.dma_start(y_rows[:, :, cols], y[:])
-            return y
+            return y[:]
 
         def round_y(cols, y, copy=nc.vector.tensor_copy):
             width = cols.stop - cols.start
             rounded = ring.tile([P, width, PACK], BF16, name="yb%d" % cols.start, tag="rounded", bufs=3, align_bytes=64)
-            copy(rounded[:].rearrange("p (c i) t -> p c t i", i=4), y[:].rearrange("p t (c i) -> p c t i", i=4))
+            copy(rounded[:].rearrange("p (c i) t -> p c t i", i=4), y.rearrange("p t (c i) -> p c t i", i=4))
             return rounded
 
         def quantize_y(cols, rounded):
@@ -356,8 +364,10 @@ def tile_list_chess_feature_value_kernel(
         r1 = round_y(c1, y1)
         quantize_y(c0, r0)
         y2 = second_stage(c2, w2_mx)
-        y3 = second_stage(c3, w2_mx)
-        y4 = second_stage(c4, w2_mx)
+        y_late = ring.tile([P, PACK, 256], F32, name="y_late", tag="y", bufs=4)
+        y3 = second_stage(c3, w2_mx, 0, y_late[:, :, 0:128])
+        y4 = second_stage(c4, w2_mx, 0, y_late[:, :, 128:256])
+        nc.sync.dma_start(y_rows[:, :, late], y_late[:])
         quantize_y(c1, r1)
         store_codes(slice(0, 512))
         r2 = round_y(c2, y2)

@@ -65,10 +65,10 @@ def tile_list_chess_feature_value_kernel(
         def load_wp(g, a, tag):
             return load_weight(wp[a * PASS : (a + 1) * PASS, g * PASS : (g + 1) * PASS], "raw_wp%d%d" % (g, a), tag)
 
-        def pick(a, words, tag, parts=1):
+        def pick(a, words, tag, widths=(S,)):
             picked[a] = slot([P, S], U32, "picked%d" % a, tag)
-            width = S // parts
-            for c0 in range(0, S, width):
+            for i, width in enumerate(widths):
+                c0 = sum(widths[:i])
                 nc.vector.tensor_copy(
                     picked[a][:, c0 : c0 + width], words[:].indirect(offsets[:, c0 // 16 : (c0 + width) // 16])
                 )
@@ -159,6 +159,13 @@ def tile_list_chess_feature_value_kernel(
                 nc.vector.tensor_copy(dst, src)
             return dealt
 
+        def round_rows(raw, name, tag):
+            woven = slot([P, PACK * PASS], BF16, name, tag)
+            nc.vector.tensor_copy(
+                woven[:].rearrange("p (c i j) -> p c j i", i=4, j=PACK), raw[:].rearrange("p j (c i) -> p c j i", i=4)
+            )
+            return woven
+
         def quantize_weight(dealt, name, parts, tags=None):
             tags = tags or (name + "_codes", name + "_plane")
             codes = slot([P, PASS], U32, name + "_codes", tags[0])
@@ -173,8 +180,8 @@ def tile_list_chess_feature_value_kernel(
                 )
             return codes, plane
 
-        def first_pass(bank, g, t, half, a, weights, start, stop):
-            cols = slice(half * BANK, (half + 1) * BANK)
+        def first_pass(bank, g, t, half, a, weights, start, stop, cols=None):
+            cols = cols or slice(half * BANK, (half + 1) * BANK)
             if a == THREAT:
                 c0 = g * PASS + t * P
                 lhs = wt_dealt[:, 2 * c0 : 2 * (c0 + P)].bitcast(E2M1)
@@ -184,7 +191,7 @@ def tile_list_chess_feature_value_kernel(
                 lhs = codes[:, t * P : (t + 1) * P].bitcast(E4M3)
                 lhs_scale = plane[:, t * P : (t + 1) * P]
             nc.tensor.matmul_mx(
-                out=bank[:],
+                out=bank,
                 lhsT=lhs,
                 lhsT_scale=lhs_scale,
                 rhs=picked[a][:, cols].bitcast(E4M3),
@@ -192,6 +199,18 @@ def tile_list_chess_feature_value_kernel(
                 start=start,
                 stop=stop,
             )
+
+        def quartered_pass(banks, g, half, quarter, t, a, weights, first, last):
+            c0 = half * BANK + quarter * CHUNK
+            out = banks[2 * quarter + t // 2][:, (t % 2) * CHUNK : (t % 2 + 1) * CHUNK]
+            first_pass(out, g, t, half, a, weights, first and t % 2 == 0, last and t % 2 == 1, slice(c0, c0 + CHUNK))
+
+        def group0_passes(banks0, a, weights, first, last):
+            for quarter in range(2):
+                for t in range(PACK):
+                    quartered_pass(banks0[0], 0, 0, quarter, t, a, weights, first, last)
+            for t in range(PACK):
+                first_pass(banks0[1][t][:], 0, t, 1, a, weights, first, last)
 
         def rectify(g, half, banks):
             rectified = ring.tile([P, PACK, BANK], F32, name="rect%d%d" % (g, half), tag="rectified", bufs=3)
@@ -202,6 +221,17 @@ def tile_list_chess_feature_value_kernel(
                 )
             return rectified
 
+        def rectify_quarter(g, rectified, quarter, banks):
+            for t in range(PACK):
+                column = slice(g * PACK + t, g * PACK + t + 1)
+                nc.scalar.activation(
+                    rectified[:, t, quarter * CHUNK : (quarter + 1) * CHUNK],
+                    banks[2 * quarter + t // 2][:, (t % 2) * CHUNK : (t % 2 + 1) * CHUNK],
+                    ACT.Relu,
+                    bias=root_bias[:, column],
+                    scale=root[:, column],
+                )
+
         h_codes = [keep.tile([P, S], U32, name="h_codes%d" % g, align_bytes=64) for g in range(2)]
         h_plane = [keep.tile([P, S], U8, name="h_plane%d" % g, align_bytes=64) for g in range(2)]
 
@@ -210,7 +240,7 @@ def tile_list_chess_feature_value_kernel(
             c0 = cols.start % BANK
             name = "hid%d_%d" % (g, cols.start)
             if tag is None:
-                hidden = ring.tile([P, width, PACK], BF16, name=name, tag="hidden", bufs=4, align_bytes=64)
+                hidden = ring.tile([P, width, PACK], BF16, name=name, tag="hidden", bufs=7, align_bytes=64)
             else:
                 hidden = slot([P, width, PACK], BF16, name, tag)
             nc.scalar.activation(
@@ -225,12 +255,19 @@ def tile_list_chess_feature_value_kernel(
                 hidden[:], hidden[:], ceiling[:, g : g + 1, :].to_broadcast(list(hidden.shape)), ALU.min
             )
 
+        def cap_into(g, hidden, name, tag):
+            capped = slot(list(hidden.shape), BF16, name, tag)
+            nc.vector.tensor_tensor(
+                capped[:], hidden[:], ceiling[:, g : g + 1, :].to_broadcast(list(hidden.shape)), ALU.min
+            )
+            return capped
+
         def sign_weight(g, dealt):
             signed = ring.tile([P, PASS, PACK], BF16, name="signed%d" % g, tag="signed", bufs=2, align_bytes=64)
             nc.vector.tensor_tensor(
-                signed[:],
-                dealt[:].rearrange("p (c j) -> p c j", j=PACK),
-                signs[:, g : g + 1, :].to_broadcast([P, PASS, PACK]),
+                signed[:].rearrange("p (t m) j -> p t m j", t=PACK),
+                dealt[:].rearrange("p (m t j) -> p t m j", t=PACK, j=PACK),
+                signs[:, g : g + 1, :].unsqueeze(1).to_broadcast([P, PACK, P, PACK]),
                 ALU.mult,
             )
             return signed[:].rearrange("p c j -> p (c j)")
@@ -295,33 +332,32 @@ def tile_list_chess_feature_value_kernel(
 
         banks0 = [open_banks(0, half) for half in range(2)]
         weights = quantize_weight(round_weight(raw_wp[0, 0], "wp00", True, "H"), "wp00", 1)
-        for half in range(2):
-            for t in range(PACK):
-                first_pass(banks0[half][t], 0, t, half, 0, weights, True, False)
+        group0_passes(banks0, 0, weights, True, False)
         pick(THREAT, table_threat, "D")
-        raw_wp[1, 1] = load_wp(1, 1, AT_WP11)
-        raw_w2 = [load_weight(w2[0:PASS, :], "raw_w20", AT_W20)]
+        raw_w2 = [load_weight(w2[0:PASS, :], "raw_w20", AT_WP11)]
+        raw_wp[1, 1] = load_wp(1, 1, AT_W20)
         nc.vector.tensor_copy(
             wt_plane[:].rearrange("p (g t m) -> p g m t", g=2, t=PACK),
             wt_scales_raw[:].rearrange("p (g m t) -> p g m t", g=2, t=PACK),
         )
-        for half in range(2):
-            for t in range(PACK):
-                first_pass(banks0[half][t], 0, t, half, THREAT, None, False, False)
+        group0_passes(banks0, THREAT, None, False, False)
         weights = quantize_weight(round_weight(raw_wp[0, 1], "wp01", True, "I"), "wp01", 1, ("wp01_codes", "W"))
         raw_w2.append(load_weight(w2[PASS : 2 * PASS, :], "raw_w21", AT_WP01))
-        pick(1, table_1, "I", 2)
-        for half in range(2):
-            for t in range(PACK):
-                first_pass(banks0[half][t], 0, t, half, 1, weights, False, True)
+        pick(1, table_1, "I", (CHUNK, CHUNK, BANK))
+        group0_passes(banks0, 1, weights, False, True)
         chunks = [slice(0, 256), slice(256, 512), slice(512, 768), slice(768, 896), slice(896, 1024)]
         c0, c1, c2, c3, c4 = chunks
         late = slice(768, 1024)
-        rect00 = rectify(0, 0, banks0[0])
+        rect00 = ring.tile([P, PACK, BANK], F32, name="rect00", tag="rectified", bufs=3)
+        for quarter in range(2):
+            rectify_quarter(0, rect00, quarter, banks0[0])
         dealt = round_weight(raw_wp[1, 0], "wp10", False, AT_TABLE1)
         wp1 = [quantize_weight(dealt, "wp10", 1)]
-        dealt = round_weight(raw_wp[1, 1], "wp11", False, AT_WP10)
-        wp1.append(quantize_weight(dealt, "wp11", 1))
+        dealt0 = round_rows(raw_w2[0], "w20", AT_WP10)
+        signed0 = sign_weight(0, dealt0)
+        dealt11 = round_weight(raw_wp[1, 1], "wp11", False, AT_WP11)
+        w2_mx = [quantize_weight(signed0, "w20", 1)]
+        wp1.append(quantize_weight(dealt11, "wp11", 1))
         h00 = finish_hidden(0, slice(0, 512), rect00, "F")
         rect01 = rectify(0, 1, banks0[1])
         h01 = finish_hidden(0, slice(512, 1024), rect01, "G")
@@ -330,14 +366,11 @@ def tile_list_chess_feature_value_kernel(
             banks1.append(open_banks(1, half))
             for t in range(PACK):
                 for a in (THREAT, 0, 1):
-                    first_pass(banks1[half][t], 1, t, half, a, None if a == THREAT else wp1[a], a == THREAT, a == 1)
-        dealt0 = round_weight(raw_w2[0], "w20", False, AT_WP11)
-        cap_hidden(0, h00)
-        signed0 = sign_weight(0, dealt0)
-        quantize_hidden(0, slice(0, 512), h00)
-        dealt1 = round_weight(raw_w2[1], "w21", False, AT_W20)
-        w2_mx = [quantize_weight(signed0, "w20", 1)]
+                    first_pass(banks1[half][t][:], 1, t, half, a, None if a == THREAT else wp1[a], a == THREAT, a == 1)
+        dealt1 = round_rows(raw_w2[1], "w21", AT_W20 + 4 * KIB)
+        h00 = cap_into(0, h00, "capped00", AT_W20)
         signed1 = sign_weight(1, dealt1)
+        quantize_hidden(0, slice(0, 512), h00)
         rect10 = rectify(1, 0, banks1[0])
         h10 = finish_hidden(1, c0, rect10)
         h11 = finish_hidden(1, c1, rect10)

@@ -28,13 +28,15 @@ AT_THREAT = 0
 AT_WP11 = 0
 AT_W20 = 8 * KIB
 AT_WT = 16 * KIB - 64
-AT_WP01 = 18 * KIB - 128
+AT_WP00 = 18 * KIB - 128
 AT_WP10 = 26 * KIB
 AT_TABLE0 = 34 * KIB - 64
 AT_TABLE1 = 34 * KIB
-AT_SCALES = 50 * KIB
-AT_MAGNITUDE = 50 * KIB + 64
-AT_PICKED0 = 50 * KIB + 128
+AT_PICKED0 = 50 * KIB
+AT_SCALES = 54 * KIB - 64
+AT_MAGNITUDE = 54 * KIB + 64
+AT_POSITIVE = 54 * KIB + 128
+AT_WP01 = 58 * KIB - 128
 
 
 def tile_list_chess_feature_value_kernel(
@@ -79,28 +81,28 @@ def tile_list_chess_feature_value_kernel(
         nc.sync.dma_start(offsets[:], offs)
         table_0 = load_table(0, AT_TABLE0)
         raw_wp = {}
-        raw_wp[0, 0] = load_wp(0, 0, "L")
 
         table_scales = slot([P, T], U8, "table_scales", AT_SCALES)
         nc.vector.memset(table_scales[:].bitcast(I32), 0)
-        wt_scales_raw = slot([P, H], U8, "wt_scales_raw", "W")
-        nc.vector.memset(wt_scales_raw[:].bitcast(I32), 0)
+        wt_scales_raw = slot([P, 4, H], U8, "wt_scales_raw", "W")
+        nc.vector.memset(wt_scales_raw[:, 0, :].bitcast(I32), 0)
         picked_plane = [keep.tile([P, S], U8, name="picked_plane%d" % a, align_bytes=64) for a in range(3)]
         for a in range(3):
             nc.vector.memset(picked_plane[a][:].bitcast(I32), 0)
-        nc.scalar.dma_start(
+        nc.sync.dma_start(
             table_scales[0:P:4, :].bitcast(I32), tab_scales[0:2].rearrange("a q t -> (a q) t").bitcast(I32)
         )
-        nc.scalar.dma_start(table_scales[2:P:8, :].bitcast(I32), tab_scales[THREAT].bitcast(I32))
-        for r in range(4):
-            nc.gpsimd.dma_start(wt_scales_raw[r:P:32, :].bitcast(I32), wt_scales[0, r:16:4, :].bitcast(I32))
+        nc.sync.dma_start(table_scales[2:P:8, :].bitcast(I32), tab_scales[THREAT].bitcast(I32))
+        nc.sync.dma_start(
+            wt_scales_raw[0:4, :, :].bitcast(I32), wt_scales[0].rearrange("(q r) c -> r q c", r=4).bitcast(I32)
+        )
 
         gains_padded = keep.tile([P, 2, 2 * PACK], F32, name="gains_padded")
         gains = gains_padded[:, :, 0:PACK]
-        nc.gpsimd.dma_start(gains, gain.rearrange("(g p t) -> p g t", g=2, t=PACK))
+        nc.scalar.dma_start(gains, gain.rearrange("(g p t) -> p g t", g=2, t=PACK))
         bias_padded = keep.tile([P, 2, 2 * PACK], F32, name="bias_padded")
         bias = bias_padded[:, :, 0:PACK]
-        nc.gpsimd.dma_start(bias, bh.rearrange("(g p t) -> p g t", g=2, t=PACK))
+        nc.scalar.dma_start(bias, bh.rearrange("(g p t) -> p g t", g=2, t=PACK))
 
         wt_dealt = keep.tile([P, 2 * H], U8, name="wt_dealt", align_bytes=64)
         wt_plane = keep.tile([P, H], U8, name="wt_plane", align_bytes=64)
@@ -110,8 +112,8 @@ def tile_list_chess_feature_value_kernel(
                 wt_raw[:, 2 * g * PASS : 2 * (g + 1) * PASS].rearrange("p (m t b) -> p m t b", t=PACK, b=2),
             )
 
+        raw_wp[0, 0] = load_wp(0, 0, AT_WP00)
         table_threat = load_table(THREAT, AT_THREAT)
-        raw_wp[0, 1] = load_wp(0, 1, AT_WP01)
 
         picked_scales = keep.tile([P, S], U8, name="picked_scales", align_bytes=64)
         nc.vector.tensor_copy(picked_scales[:], table_scales[:].indirect(offsets[:]))
@@ -119,13 +121,19 @@ def tile_list_chess_feature_value_kernel(
         nc.scalar.activation(magnitude[:].rearrange("p (g t) -> p g t", g=2), gains, ACT.Abs)
         rough = keep.tile([P, 2 * PACK], F32, name="rough")
         nc.scalar.activation(rough[:], magnitude[:], ACT.Sqrt)
-        for a, queue in ((0, nc.gpsimd), (THREAT, nc.scalar), (1, nc.gpsimd)):
-            for r in range(4):
+        moves = [(a, r) for a in (0, THREAT, 1) for r in range(4)]
+
+        def move_scales(some):
+            for a, r in some:
                 rows = slice(2 + 8 * r, P, 32) if a == THREAT else slice(64 * a + 4 * r, 64 * (a + 1), 16)
-                queue.dma_start(
+                nc.sync.dma_start(
                     picked_plane[a][SCALE_ROW[a] + r : P : 32, :].bitcast(I32),
                     picked_scales[rows, :].bitcast(I32),
                 )
+
+        move_scales(moves[:6])
+        raw_wp[0, 1] = load_wp(0, 1, AT_WP01)
+        move_scales(moves[6:])
         picked = {}
         pick(0, table_0, AT_PICKED0)
         table_1 = load_table(1, AT_TABLE1)
@@ -142,7 +150,7 @@ def tile_list_chess_feature_value_kernel(
         )
         ceiling = keep.tile([P, 2, PACK], BF16, name="ceiling")
         nc.vector.tensor_copy(ceiling[:].rearrange("p g t -> p (g t)"), magnitude[:])
-        positive = slot([P, 2, PACK], F32, "positive", AT_SCALES)
+        positive = slot([P, 2, PACK], F32, "positive", AT_POSITIVE)
         nc.vector.tensor_scalar(positive[:], gains, 0.0, None, ALU.is_ge)
         signs = keep.tile([P, 2, PACK], BF16, name="signs")
         nc.vector.tensor_scalar(signs[:], positive[:], 2.0, -1.0, ALU.mult, ALU.add)
@@ -336,9 +344,13 @@ def tile_list_chess_feature_value_kernel(
         pick(THREAT, table_threat, "D")
         raw_w2 = [load_weight(w2[0:PASS, :], "raw_w20", AT_WP11)]
         raw_wp[1, 1] = load_wp(1, 1, AT_W20)
+        for q in range(1, 4):
+            nc.vector.tensor_copy(
+                wt_scales_raw[32 * q : 32 * q + 4, 0, :].bitcast(I32), wt_scales_raw[0:4, q, :].bitcast(I32)
+            )
         nc.vector.tensor_copy(
             wt_plane[:].rearrange("p (g t m) -> p g m t", g=2, t=PACK),
-            wt_scales_raw[:].rearrange("p (g m t) -> p g m t", g=2, t=PACK),
+            wt_scales_raw[:, 0, :].rearrange("p (g m t) -> p g m t", g=2, t=PACK),
         )
         group0_passes(banks0, THREAT, None, False, False)
         weights = quantize_weight(round_weight(raw_wp[0, 1], "wp01", True, "I"), "wp01", 1, ("wp01_codes", "W"))

@@ -84,7 +84,7 @@ def tile_list_chess_feature_value_kernel(
 
         table_scales = slot([P, T], U8, "table_scales", AT_SCALES)
         nc.vector.memset(table_scales[:].bitcast(I32), 0)
-        wt_scales_raw = slot([P, 4, H], U8, "wt_scales_raw", "W")
+        wt_scales_raw = slot([P, 2, H], U8, "wt_scales_raw", "W")
         nc.vector.memset(wt_scales_raw[:, 0, :].bitcast(I32), 0)
         picked_plane = [keep.tile([P, S], U8, name="picked_plane%d" % a, align_bytes=64) for a in range(3)]
         for a in range(3):
@@ -92,10 +92,12 @@ def tile_list_chess_feature_value_kernel(
         nc.sync.dma_start(
             table_scales[0:P:4, :].bitcast(I32), tab_scales[0:2].rearrange("a q t -> (a q) t").bitcast(I32)
         )
-        nc.sync.dma_start(table_scales[2:P:8, :].bitcast(I32), tab_scales[THREAT].bitcast(I32))
-        nc.sync.dma_start(
-            wt_scales_raw[0:4, :, :].bitcast(I32), wt_scales[0].rearrange("(q r) c -> r q c", r=4).bitcast(I32)
-        )
+        nc.sync.dma_start(table_scales[6:P:8, :].bitcast(I32), tab_scales[THREAT].bitcast(I32))
+        for half in range(2):
+            nc.sync.dma_start(
+                wt_scales_raw[64 * half : 64 * half + 4, :, :].bitcast(I32),
+                wt_scales[0, 8 * half : 8 * half + 8, :].rearrange("(q r) c -> r q c", r=4).bitcast(I32),
+            )
 
         gains_padded = keep.tile([P, 2, 2 * PACK], F32, name="gains_padded")
         gains = gains_padded[:, :, 0:PACK]
@@ -125,7 +127,7 @@ def tile_list_chess_feature_value_kernel(
 
         def move_scales(some):
             for a, r in some:
-                rows = slice(2 + 8 * r, P, 32) if a == THREAT else slice(64 * a + 4 * r, 64 * (a + 1), 16)
+                rows = slice(6 + 8 * r, P, 32) if a == THREAT else slice(64 * a + 4 * r, 64 * (a + 1), 16)
                 nc.sync.dma_start(
                     picked_plane[a][SCALE_ROW[a] + r : P : 32, :].bitcast(I32),
                     picked_scales[rows, :].bitcast(I32),
@@ -344,9 +346,10 @@ def tile_list_chess_feature_value_kernel(
         pick(THREAT, table_threat, "D")
         raw_w2 = [load_weight(w2[0:PASS, :], "raw_w20", AT_WP11)]
         raw_wp[1, 1] = load_wp(1, 1, AT_W20)
-        for q in range(1, 4):
+        for half in range(2):
             nc.vector.tensor_copy(
-                wt_scales_raw[32 * q : 32 * q + 4, 0, :].bitcast(I32), wt_scales_raw[0:4, q, :].bitcast(I32)
+                wt_scales_raw[64 * half + 32 : 64 * half + 36, 0, :].bitcast(I32),
+                wt_scales_raw[64 * half : 64 * half + 4, 1, :].bitcast(I32),
             )
         nc.vector.tensor_copy(
             wt_plane[:].rearrange("p (g t m) -> p g m t", g=2, t=PACK),

@@ -1,6 +1,7 @@
 from contextlib import ExitStack
 
 import concourse.mybir as mybir
+from concourse.masks import make_identity
 
 K, KP, KT, T, S, H, N = 1536, 1024, 512, 4096, 1024, 1024, 512
 FLOPS = 2 * K * H * S + 2 * H * N * S
@@ -23,6 +24,7 @@ BANK = 512
 CHUNK = 256
 THREAT = 2
 SCALE_ROW = {THREAT: 0, 0: 4, 1: 8}
+GAIN_ROW, BIAS_ROW = 16, 24
 KIB = 1024
 AT_THREAT = 0
 AT_WP11 = 0
@@ -99,12 +101,20 @@ def tile_list_chess_feature_value_kernel(
                 wt_scales[0, 8 * half : 8 * half + 8, :].rearrange("(q r) c -> r q c", r=4).bitcast(I32),
             )
 
-        gains_padded = keep.tile([P, 2, 2 * PACK], F32, name="gains_padded")
-        gains = gains_padded[:, :, 0:PACK]
-        nc.scalar.dma_start(gains, gain.rearrange("(g p t) -> p g t", g=2, t=PACK))
-        bias_padded = keep.tile([P, 2, 2 * PACK], F32, name="bias_padded")
-        bias = bias_padded[:, :, 0:PACK]
-        nc.scalar.dma_start(bias, bh.rearrange("(g p t) -> p g t", g=2, t=PACK))
+        rows_in = keep.tile([P, H], F32, name="rows_in")
+        nc.gpsimd.memset(rows_in[:], 0.0)
+        nc.scalar.dma_start(rows_in[GAIN_ROW : GAIN_ROW + 1, :], gain.unsqueeze(0))
+        nc.scalar.dma_start(rows_in[BIAS_ROW : BIAS_ROW + 1, :], bh.unsqueeze(0))
+        identity = keep.tile([P, P], F32, name="identity")
+        make_identity(nc, identity[:])
+        turned = keep.tile([P, 2, PACK, 2], F32, name="turned")
+        for g in range(2):
+            bank = psum.tile([P, PACK, P], F32, name="turn%d" % g, tag="bank")
+            for t in range(PACK):
+                nc.tensor.transpose(bank[:, t, :], rows_in[:, g * PASS + t : (g + 1) * PASS : PACK], identity[:])
+            nc.vector.tensor_copy(turned[:, g, :, :], bank[:, :, GAIN_ROW : BIAS_ROW + 1 : BIAS_ROW - GAIN_ROW])
+        gains = turned[:, :, :, 0]
+        bias = turned[:, :, :, 1]
 
         wt_dealt = keep.tile([P, 2 * H], U8, name="wt_dealt", align_bytes=64)
         wt_plane = keep.tile([P, H], U8, name="wt_plane", align_bytes=64)
@@ -135,10 +145,11 @@ def tile_list_chess_feature_value_kernel(
 
         move_scales(moves[:6])
         raw_wp[0, 1] = load_wp(0, 1, AT_WP01)
-        move_scales(moves[6:])
+        move_scales(moves[6:8])
         picked = {}
         pick(0, table_0, AT_PICKED0)
         table_1 = load_table(1, AT_TABLE1)
+        move_scales(moves[8:])
         inverse = keep.tile([P, 2 * PACK], F32, name="inverse")
         nc.vector.tensor_scalar(inverse[:], rough[:], 1e-30, None, ALU.max)
         nc.vector.reciprocal(inverse[:], inverse[:])

@@ -30,9 +30,10 @@ AT_THREAT = 0
 AT_WP11 = 0
 AT_W20 = 8 * KIB
 AT_WT = 16 * KIB - 64
-AT_WP00 = 18 * KIB - 128
-AT_WP10 = 26 * KIB
-AT_TABLE0 = 34 * KIB - 64
+AT_WT_LATE = 33 * KIB
+AT_WP00 = 17 * KIB - 128
+AT_WP10 = 25 * KIB
+AT_TABLE0 = 33 * KIB - 64
 AT_TABLE1 = 34 * KIB
 AT_PICKED0 = 50 * KIB
 AT_SCALES = 54 * KIB - 64
@@ -49,7 +50,7 @@ def tile_list_chess_feature_value_kernel(
         keep = ctx.enter_context(tc.tile_pool(name="keep", bufs=1))
         ring = ctx.enter_context(tc.tile_pool(name="ring", bufs=1))
         lap = ctx.enter_context(tc.tile_pool(name="lap", bufs=1))
-        psum = ctx.enter_context(tc.psum_pool(name="psum", bufs=8))
+        psum = ctx.enter_context(tc.psum_pool(name="psum", bufs=1))
 
         def slot(shape, dtype, name, tag):
             if isinstance(tag, int):
@@ -77,8 +78,8 @@ def tile_list_chess_feature_value_kernel(
                     picked[a][:, c0 : c0 + width], words[:].indirect(offsets[:, c0 // 16 : (c0 + width) // 16])
                 )
 
-        wt_raw = slot([P, 2 * H], U8, "wt_raw", AT_WT)
-        nc.sync.dma_start(wt_raw[:].bitcast(I32), wt_words[0].bitcast(I32))
+        wt_raw = slot([P, H], U8, "wt_raw", AT_WT)
+        nc.sync.dma_start(wt_raw[:].bitcast(I32), wt_words[0][:, 0:H].bitcast(I32))
         offsets = keep.tile([P, S // 16], U16, name="offsets")
         nc.sync.dma_start(offsets[:], offs)
         table_0 = load_table(0, AT_TABLE0)
@@ -109,20 +110,19 @@ def tile_list_chess_feature_value_kernel(
         make_identity(nc, identity[:])
         turned = keep.tile([P, 2, PACK, 2], F32, name="turned")
         for g in range(2):
-            bank = psum.tile([P, PACK, P], F32, name="turn%d" % g, tag="bank")
+            bank = psum.tile([P, PACK, P], F32, name="turn%d" % g, tag="bank%d" % g)
             for t in range(PACK):
                 nc.tensor.transpose(bank[:, t, :], rows_in[:, g * PASS + t : (g + 1) * PASS : PACK], identity[:])
             nc.vector.tensor_copy(turned[:, g, :, :], bank[:, :, GAIN_ROW : BIAS_ROW + 1 : BIAS_ROW - GAIN_ROW])
         gains = turned[:, :, :, 0]
         bias = turned[:, :, :, 1]
 
-        wt_dealt = keep.tile([P, 2 * H], U8, name="wt_dealt", align_bytes=64)
+        wt_dealt = [keep.tile([P, H], U8, name="wt_dealt%d" % g, align_bytes=64) for g in range(2)]
         wt_plane = keep.tile([P, H], U8, name="wt_plane", align_bytes=64)
-        for g in range(2):
-            nc.vector.tensor_copy(
-                wt_dealt[:, 2 * g * PASS : 2 * (g + 1) * PASS].rearrange("p (t m b) -> p m t b", t=PACK, b=2),
-                wt_raw[:, 2 * g * PASS : 2 * (g + 1) * PASS].rearrange("p (m t b) -> p m t b", t=PACK, b=2),
-            )
+        nc.vector.tensor_copy(
+            wt_dealt[0][:].rearrange("p (t m b) -> p m t b", t=PACK, b=2),
+            wt_raw[:].rearrange("p (m t b) -> p m t b", t=PACK, b=2),
+        )
 
         raw_wp[0, 0] = load_wp(0, 0, AT_WP00)
         table_threat = load_table(THREAT, AT_THREAT)
@@ -149,6 +149,8 @@ def tile_list_chess_feature_value_kernel(
         picked = {}
         pick(0, table_0, AT_PICKED0)
         table_1 = load_table(1, AT_TABLE1)
+        wt_late = slot([P, H], U8, "wt_late", AT_WT_LATE)
+        nc.sync.dma_start(wt_late[:].bitcast(I32), wt_words[0][:, H : 2 * H].bitcast(I32))
         move_scales(moves[8:])
         inverse = keep.tile([P, 2 * PACK], F32, name="inverse")
         nc.vector.tensor_scalar(inverse[:], rough[:], 1e-30, None, ALU.max)
@@ -205,7 +207,7 @@ def tile_list_chess_feature_value_kernel(
             cols = cols or slice(half * BANK, (half + 1) * BANK)
             if a == THREAT:
                 c0 = g * PASS + t * P
-                lhs = wt_dealt[:, 2 * c0 : 2 * (c0 + P)].bitcast(E2M1)
+                lhs = wt_dealt[g][:, 2 * t * P : 2 * (t + 1) * P].bitcast(E2M1)
                 lhs_scale = wt_plane[:, c0 : c0 + P]
             else:
                 codes, plane = weights
@@ -305,10 +307,13 @@ def tile_list_chess_feature_value_kernel(
         y_rows = out_0.rearrange("(p t) j -> p t j", t=PACK)
         y_words = out_1[0].rearrange("p m t -> p (m t)").bitcast(I32)
 
-        def second_stage(cols, w2_mx, on_vector=0, into=None):
+        def second_stage(cols, w2_mx, first_bank, on_vector=0, into=None):
             width = cols.stop - cols.start
             side = BANK // width
-            banks = [psum.tile([P, BANK], F32, name="ybank%d_%d" % (cols.start, b), tag="bank") for b in range(PACK // side)]
+            banks = [
+                psum.tile([P, BANK], F32, name="ybank%d_%d" % (cols.start, b), tag="bank%d" % (first_bank + b))
+                for b in range(PACK // side)
+            ]
             for g in range(2):
                 codes, plane = w2_mx[g]
                 for t in range(PACK):
@@ -349,7 +354,10 @@ def tile_list_chess_feature_value_kernel(
             nc.sync.dma_start(y_words[:, cols], y_codes[:, cols].bitcast(I32))
 
         def open_banks(g, half):
-            return [psum.tile([P, BANK], F32, name="bank%d%d%d" % (g, half, t), tag="bank") for t in range(PACK)]
+            return [
+                psum.tile([P, BANK], F32, name="bank%d%d%d" % (g, half, t), tag="bank%d" % (PACK * half + t))
+                for t in range(PACK)
+            ]
 
         banks0 = [open_banks(0, half) for half in range(2)]
         weights = quantize_weight(round_weight(raw_wp[0, 0], "wp00", True, "H"), "wp00", 1)
@@ -374,6 +382,10 @@ def tile_list_chess_feature_value_kernel(
         chunks = [slice(0, 256), slice(256, 512), slice(512, 768), slice(768, 896), slice(896, 1024)]
         c0, c1, c2, c3, c4 = chunks
         late = slice(768, 1024)
+        nc.scalar.copy(
+            wt_dealt[1][:].bitcast(U16).rearrange("p (t m) -> p m t", t=PACK),
+            wt_late[:].bitcast(U16).rearrange("p (m t) -> p m t", t=PACK),
+        )
         rect00 = ring.tile([P, PACK, BANK], F32, name="rect00", tag="rectified", bufs=3)
         for quarter in range(2):
             rectify_quarter(0, rect00, quarter, banks0[0])
@@ -408,11 +420,11 @@ def tile_list_chess_feature_value_kernel(
         quantize_hidden(1, c1, h11)
         quantize_hidden(0, slice(512, 1024), h01)
         rect11 = rectify(1, 1, banks1[1])
-        y0 = second_stage(c0, w2_mx, 2)
+        y0 = second_stage(c0, w2_mx, 0, 2)
         h12 = finish_hidden(1, c2, rect11)
         cap_hidden(1, h12)
         quantize_hidden(1, c2, h12)
-        y1 = second_stage(c1, w2_mx)
+        y1 = second_stage(c1, w2_mx, 2)
         h13 = finish_hidden(1, c3, rect11)
         cap_hidden(1, h13)
         quantize_hidden(1, c3, h13)
@@ -422,10 +434,10 @@ def tile_list_chess_feature_value_kernel(
         r0 = round_y(c0, y0)
         r1 = round_y(c1, y1)
         quantize_y(c0, r0)
-        y2 = second_stage(c2, w2_mx)
+        y2 = second_stage(c2, w2_mx, 4)
         y_late = ring.tile([P, PACK, 256], F32, name="y_late", tag="y", bufs=4)
-        y3 = second_stage(c3, w2_mx, 0, y_late[:, :, 0:128])
-        y4 = second_stage(c4, w2_mx, 0, y_late[:, :, 128:256])
+        y3 = second_stage(c3, w2_mx, 6, 0, y_late[:, :, 0:128])
+        y4 = second_stage(c4, w2_mx, 7, 0, y_late[:, :, 128:256])
         nc.sync.dma_start(y_rows[:, :, late], y_late[:])
         quantize_y(c1, r1)
         store_codes(slice(0, 512))

@@ -403,8 +403,10 @@ def tile_list_chess_feature_value_kernel(
         for half in range(2):
             banks1.append(open_banks(1, half))
             for t in range(PACK):
-                for a in (THREAT, 0, 1):
-                    first_pass(banks1[half][t][:], 1, t, half, a, None if a == THREAT else wp1[a], a == THREAT, a == 1)
+                order = (1, THREAT, 0) if half and t >= 2 else (THREAT, 0, 1)
+                for a in order:
+                    weights = None if a == THREAT else wp1[a]
+                    first_pass(banks1[half][t][:], 1, t, half, a, weights, a == order[0], a == order[-1])
         dealt1 = round_rows(raw_w2[1], "w21", AT_W20 + 4 * KIB)
         h00 = cap_into(0, h00, "capped00", AT_W20)
         signed1 = sign_weight(1, dealt1)
@@ -436,8 +438,8 @@ def tile_list_chess_feature_value_kernel(
         quantize_y(c0, r0)
         y2 = second_stage(c2, w2_mx, 4)
         y_late = ring.tile([P, PACK, 256], F32, name="y_late", tag="y", bufs=4)
-        y3 = second_stage(c3, w2_mx, 6, 0, y_late[:, :, 0:128])
-        y4 = second_stage(c4, w2_mx, 7, 0, y_late[:, :, 128:256])
+        y3 = second_stage(c3, w2_mx, 0, 0, y_late[:, :, 0:128])
+        y4 = second_stage(c4, w2_mx, 1, 0, y_late[:, :, 128:256])
         nc.sync.dma_start(y_rows[:, :, late], y_late[:])
         quantize_y(c1, r1)
         store_codes(slice(0, 512))

@@ -26,20 +26,23 @@ THREAT = 2
 SCALE_ROW = {THREAT: 0, 0: 4, 1: 8}
 GAIN_ROW, BIAS_ROW = 16, 24
 KIB = 1024
-AT_THREAT = 0
 AT_WP11 = 0
-AT_W20 = 8 * KIB
-AT_WT = 16 * KIB - 64
-AT_WT_LATE = 33 * KIB
-AT_WP00 = 17 * KIB - 128
-AT_WP10 = 25 * KIB
-AT_TABLE0 = 33 * KIB - 64
-AT_TABLE1 = 34 * KIB
-AT_PICKED0 = 50 * KIB
-AT_SCALES = 54 * KIB - 64
-AT_MAGNITUDE = 54 * KIB + 64
-AT_POSITIVE = 54 * KIB + 128
-AT_WP01 = 58 * KIB - 128
+AT_TABLE1 = 8 * KIB - 64
+AT_WT1 = 8 * KIB
+AT_WP10 = 9 * KIB
+AT_W20 = 17 * KIB
+AT_DIAGONAL = 24 * KIB - 256
+AT_WP00 = 24 * KIB
+AT_TABLE0 = 32 * KIB
+AT_INVERSE = 32 * KIB
+AT_WT0 = 32 * KIB + 64
+AT_THREAT_PLANE = 33 * KIB + 64
+AT_THREAT = 34 * KIB + 64
+AT_W21 = 38 * KIB + 64
+AT_PICKED0 = 50 * KIB + 64
+AT_SCALES = 54 * KIB
+AT_POSITIVE = 55 * KIB
+AT_WP01 = 58 * KIB - 64
 
 
 def tile_list_chess_feature_value_kernel(
@@ -78,8 +81,6 @@ def tile_list_chess_feature_value_kernel(
                     picked[a][:, c0 : c0 + width], words[:].indirect(offsets[:, c0 // 16 : (c0 + width) // 16])
                 )
 
-        wt_raw = slot([P, H], U8, "wt_raw", AT_WT)
-        nc.sync.dma_start(wt_raw[:].bitcast(I32), wt_words[0][:, 0:H].bitcast(I32))
         offsets = keep.tile([P, S // 16], U16, name="offsets")
         nc.sync.dma_start(offsets[:], offs)
         table_0 = load_table(0, AT_TABLE0)
@@ -89,8 +90,8 @@ def tile_list_chess_feature_value_kernel(
         nc.vector.memset(table_scales[:].bitcast(I32), 0)
         wt_scales_raw = slot([P, 2, H], U8, "wt_scales_raw", "W")
         nc.vector.memset(wt_scales_raw[:, 0, :].bitcast(I32), 0)
-        picked_plane = [keep.tile([P, S], U8, name="picked_plane%d" % a, align_bytes=64) for a in range(3)]
-        for a in range(3):
+        picked_plane = [keep.tile([P, S], U8, name="picked_plane%d" % a, align_bytes=64) for a in range(2)]
+        for a in range(2):
             nc.vector.memset(picked_plane[a][:].bitcast(I32), 0)
         nc.sync.dma_start(
             table_scales[0:P:4, :].bitcast(I32), tab_scales[0:2].rearrange("a q t -> (a q) t").bitcast(I32)
@@ -107,33 +108,31 @@ def tile_list_chess_feature_value_kernel(
         nc.scalar.dma_start(rows_in[GAIN_ROW : GAIN_ROW + 1, :], gain.unsqueeze(0))
         nc.scalar.dma_start(rows_in[BIAS_ROW : BIAS_ROW + 1, :], bh.unsqueeze(0))
         identity = keep.tile([P, P], F32, name="identity")
-        make_identity(nc, identity[:])
+        diagonal = slot([P, P], F32, "diagonal", AT_DIAGONAL)
+        make_identity(nc, diagonal[:])
+        nc.vector.tensor_copy(identity[:], diagonal[:])
         turned = keep.tile([P, 2, PACK, 2], F32, name="turned")
         for g in range(2):
             bank = psum.tile([P, PACK, P], F32, name="turn%d" % g, tag="bank%d" % g)
             for t in range(PACK):
                 nc.tensor.transpose(bank[:, t, :], rows_in[:, g * PASS + t : (g + 1) * PASS : PACK], identity[:])
-            nc.vector.tensor_copy(turned[:, g, :, :], bank[:, :, GAIN_ROW : BIAS_ROW + 1 : BIAS_ROW - GAIN_ROW])
+            nc.scalar.copy(turned[:, g, :, :], bank[:, :, GAIN_ROW : BIAS_ROW + 1 : BIAS_ROW - GAIN_ROW])
         gains = turned[:, :, :, 0]
         bias = turned[:, :, :, 1]
 
         wt_dealt = [keep.tile([P, H], U8, name="wt_dealt%d" % g, align_bytes=64) for g in range(2)]
         wt_plane = keep.tile([P, H], U8, name="wt_plane", align_bytes=64)
-        nc.vector.tensor_copy(
-            wt_dealt[0][:].rearrange("p (t m b) -> p m t b", t=PACK, b=2),
-            wt_raw[:].rearrange("p (m t b) -> p m t b", t=PACK, b=2),
-        )
 
         raw_wp[0, 0] = load_wp(0, 0, AT_WP00)
-        table_threat = load_table(THREAT, AT_THREAT)
+        table_1 = load_table(1, AT_TABLE1)
 
         picked_scales = keep.tile([P, S], U8, name="picked_scales", align_bytes=64)
         nc.vector.tensor_copy(picked_scales[:], table_scales[:].indirect(offsets[:]))
-        magnitude = slot([P, 2 * PACK], F32, "magnitude", AT_MAGNITUDE)
+        magnitude = keep.tile([P, 2 * PACK], F32, name="magnitude")
         nc.scalar.activation(magnitude[:].rearrange("p (g t) -> p g t", g=2), gains, ACT.Abs)
         rough = keep.tile([P, 2 * PACK], F32, name="rough")
         nc.scalar.activation(rough[:], magnitude[:], ACT.Sqrt)
-        moves = [(a, r) for a in (0, THREAT, 1) for r in range(4)]
+        moves = [(a, r) for a in (0, 1, THREAT) for r in range(4)]
 
         def move_scales(some):
             for a, r in some:
@@ -143,16 +142,25 @@ def tile_list_chess_feature_value_kernel(
                     picked_scales[rows, :].bitcast(I32),
                 )
 
+        def load_wt(g, tag):
+            raw = slot([P, H], U8, "wt_raw%d" % g, tag)
+            nc.sync.dma_start(raw[:].bitcast(I32), wt_words[0][:, g * H : (g + 1) * H].bitcast(I32))
+            return raw
+
+        def deal_wt(g, raw, tiles):
+            nc.scalar.copy(
+                wt_dealt[g][:].bitcast(U16).rearrange("p (t m) -> p m t", t=PACK)[:, :, tiles],
+                raw[:].bitcast(U16).rearrange("p (m t) -> p m t", t=PACK)[:, :, tiles],
+            )
+
         move_scales(moves[:6])
         raw_wp[0, 1] = load_wp(0, 1, AT_WP01)
         move_scales(moves[6:8])
         picked = {}
         pick(0, table_0, AT_PICKED0)
-        table_1 = load_table(1, AT_TABLE1)
-        wt_late = slot([P, H], U8, "wt_late", AT_WT_LATE)
-        nc.sync.dma_start(wt_late[:].bitcast(I32), wt_words[0][:, H : 2 * H].bitcast(I32))
-        move_scales(moves[8:])
-        inverse = keep.tile([P, 2 * PACK], F32, name="inverse")
+        picked_plane.append(slot([P, S], U8, "picked_plane2", AT_THREAT_PLANE))
+        nc.vector.memset(picked_plane[THREAT][:].bitcast(I32), 0)
+        inverse = slot([P, 2 * PACK], F32, "inverse", AT_INVERSE)
         nc.vector.tensor_scalar(inverse[:], rough[:], 1e-30, None, ALU.max)
         nc.vector.reciprocal(inverse[:], inverse[:])
         nc.vector.tensor_tensor(inverse[:], inverse[:], magnitude[:], ALU.mult)
@@ -170,7 +178,9 @@ def tile_list_chess_feature_value_kernel(
         signs = keep.tile([P, 2, PACK], BF16, name="signs")
         nc.vector.tensor_scalar(signs[:], positive[:], 2.0, -1.0, ALU.mult, ALU.add)
 
-        raw_wp[1, 0] = load_wp(1, 0, AT_WP10)
+        table_threat = load_table(THREAT, AT_THREAT)
+        wt_raw = [load_wt(0, AT_WT0)]
+        move_scales(moves[8:])
 
         def round_weight(raw, name, shared, tag):
             dealt = slot([P, PACK * PASS], BF16, name, tag)
@@ -180,6 +190,14 @@ def tile_list_chess_feature_value_kernel(
                 nc.scalar.copy(dst, src)
             else:
                 nc.vector.tensor_copy(dst, src)
+            return dealt
+
+        def round_shared(raw, name, tag):
+            dealt = slot([P, PACK * PASS], BF16, name, tag)
+            dst = dealt[:].rearrange("p (t m j) -> p m j t", t=PACK, j=PACK)
+            src = raw[:].rearrange("p j (m t) -> p m j t", t=PACK)
+            nc.vector.tensor_copy(dst[:, :, :, 0:2], src[:, :, :, 0:2])
+            nc.scalar.copy(dst[:, :, :, 2:4], src[:, :, :, 2:4])
             return dealt
 
         def round_rows(raw, name, tag):
@@ -362,9 +380,9 @@ def tile_list_chess_feature_value_kernel(
         banks0 = [open_banks(0, half) for half in range(2)]
         weights = quantize_weight(round_weight(raw_wp[0, 0], "wp00", True, "H"), "wp00", 1)
         group0_passes(banks0, 0, weights, True, False)
-        pick(THREAT, table_threat, "D")
-        raw_w2 = [load_weight(w2[0:PASS, :], "raw_w20", AT_WP11)]
-        raw_wp[1, 1] = load_wp(1, 1, AT_W20)
+        pick(1, table_1, "D")
+        weights = quantize_weight(round_shared(raw_wp[0, 1], "wp01", "I"), "wp01", 2)
+        group0_passes(banks0, 1, weights, False, False)
         for half in range(2):
             nc.vector.tensor_copy(
                 wt_scales_raw[64 * half + 32 : 64 * half + 36, 0, :].bitcast(I32),
@@ -374,26 +392,27 @@ def tile_list_chess_feature_value_kernel(
             wt_plane[:].rearrange("p (g t m) -> p g m t", g=2, t=PACK),
             wt_scales_raw[:, 0, :].rearrange("p (g m t) -> p g m t", g=2, t=PACK),
         )
-        group0_passes(banks0, THREAT, None, False, False)
-        weights = quantize_weight(round_weight(raw_wp[0, 1], "wp01", True, "I"), "wp01", 1, ("wp01_codes", "W"))
-        raw_w2.append(load_weight(w2[PASS : 2 * PASS, :], "raw_w21", AT_WP01))
-        pick(1, table_1, "I", (CHUNK, CHUNK, BANK))
-        group0_passes(banks0, 1, weights, False, True)
+        wt_raw.append(load_wt(1, AT_WT1))
+        raw_wp[1, 0] = load_wp(1, 0, AT_WP10)
+        raw_w2 = [load_weight(w2[0:PASS, :], "raw_w20", AT_W20)]
+        raw_wp[1, 1] = load_wp(1, 1, AT_WP11)
+        pick(THREAT, table_threat, "I", (CHUNK, CHUNK, BANK))
+        raw_w2.append(load_weight(w2[PASS : 2 * PASS, :], "raw_w21", AT_W21))
+        deal_wt(0, wt_raw[0], slice(0, 2))
+        deal_wt(0, wt_raw[0], slice(2, 4))
+        deal_wt(1, wt_raw[1], slice(0, 4))
+        group0_passes(banks0, THREAT, None, False, True)
         chunks = [slice(0, 256), slice(256, 512), slice(512, 768), slice(768, 896), slice(896, 1024)]
         c0, c1, c2, c3, c4 = chunks
         late = slice(768, 1024)
-        nc.scalar.copy(
-            wt_dealt[1][:].bitcast(U16).rearrange("p (t m) -> p m t", t=PACK),
-            wt_late[:].bitcast(U16).rearrange("p (m t) -> p m t", t=PACK),
-        )
         rect00 = ring.tile([P, PACK, BANK], F32, name="rect00", tag="rectified", bufs=3)
         for quarter in range(2):
             rectify_quarter(0, rect00, quarter, banks0[0])
-        dealt = round_weight(raw_wp[1, 0], "wp10", False, AT_TABLE1)
+        dealt = round_weight(raw_wp[1, 0], "wp10", False, AT_THREAT)
         wp1 = [quantize_weight(dealt, "wp10", 1)]
         dealt0 = round_rows(raw_w2[0], "w20", AT_WP10)
         signed0 = sign_weight(0, dealt0)
-        dealt11 = round_weight(raw_wp[1, 1], "wp11", False, AT_WP11)
+        dealt11 = round_weight(raw_wp[1, 1], "wp11", False, AT_W20)
         w2_mx = [quantize_weight(signed0, "w20", 1)]
         wp1.append(quantize_weight(dealt11, "wp11", 1))
         h00 = finish_hidden(0, slice(0, 512), rect00, "F")
@@ -407,8 +426,8 @@ def tile_list_chess_feature_value_kernel(
                 for a in order:
                     weights = None if a == THREAT else wp1[a]
                     first_pass(banks1[half][t][:], 1, t, half, a, weights, a == order[0], a == order[-1])
-        dealt1 = round_rows(raw_w2[1], "w21", AT_W20 + 4 * KIB)
-        h00 = cap_into(0, h00, "capped00", AT_W20)
+        dealt1 = round_rows(raw_w2[1], "w21", AT_WP11 + 4 * KIB)
+        h00 = cap_into(0, h00, "capped00", AT_WP11)
         signed1 = sign_weight(1, dealt1)
         quantize_hidden(0, slice(0, 512), h00)
         rect10 = rectify(1, 0, banks1[0])

@@ -29,14 +29,14 @@ KIB = 1024
 AT_WP11 = 0
 AT_TABLE1 = 8 * KIB - 64
 AT_WT1 = 8 * KIB
-AT_WP10 = 9 * KIB
-AT_W20 = 17 * KIB
+AT_W20A = 9 * KIB
+AT_WP10 = 13 * KIB
+AT_W20B = 21 * KIB
 AT_DIAGONAL = 24 * KIB - 256
 AT_WP00 = 24 * KIB
 AT_TABLE0 = 32 * KIB
 AT_INVERSE = 32 * KIB
 AT_WT0 = 32 * KIB + 64
-AT_THREAT_PLANE = 33 * KIB + 64
 AT_THREAT = 34 * KIB + 64
 AT_W21 = 38 * KIB + 64
 AT_PICKED0 = 50 * KIB + 64
@@ -73,13 +73,20 @@ def tile_list_chess_feature_value_kernel(
         def load_wp(g, a, tag):
             return load_weight(wp[a * PASS : (a + 1) * PASS, g * PASS : (g + 1) * PASS], "raw_wp%d%d" % (g, a), tag)
 
-        def pick(a, words, tag, widths=(S,)):
+        def pick_part(a, words, c0, width):
+            nc.vector.tensor_copy(
+                picked[a][:, c0 : c0 + width], words[:].indirect(offsets[:, c0 // 16 : (c0 + width) // 16])
+            )
+
+        def pick(a, words, tag):
             picked[a] = slot([P, S], U32, "picked%d" % a, tag)
-            for i, width in enumerate(widths):
-                c0 = sum(widths[:i])
-                nc.vector.tensor_copy(
-                    picked[a][:, c0 : c0 + width], words[:].indirect(offsets[:, c0 // 16 : (c0 + width) // 16])
-                )
+            pick_part(a, words, 0, S)
+
+        def load_columns(half, tag):
+            raw = slot([P, PACK, CHUNK], F32, "raw_w20%d" % half, tag)
+            rows = w2[0:PASS, half * CHUNK : (half + 1) * CHUNK]
+            nc.sync.dma_start(raw[:], rows.rearrange("(p j) c -> p j c", j=PACK))
+            return raw
 
         offsets = keep.tile([P, S // 16], U16, name="offsets")
         nc.sync.dma_start(offsets[:], offs)
@@ -90,8 +97,8 @@ def tile_list_chess_feature_value_kernel(
         nc.vector.memset(table_scales[:].bitcast(I32), 0)
         wt_scales_raw = slot([P, 2, H], U8, "wt_scales_raw", "W")
         nc.vector.memset(wt_scales_raw[:, 0, :].bitcast(I32), 0)
-        picked_plane = [keep.tile([P, S], U8, name="picked_plane%d" % a, align_bytes=64) for a in range(2)]
-        for a in range(2):
+        picked_plane = [keep.tile([P, S], U8, name="picked_plane%d" % a, align_bytes=64) for a in range(3)]
+        for a in range(3):
             nc.vector.memset(picked_plane[a][:].bitcast(I32), 0)
         nc.sync.dma_start(
             table_scales[0:P:4, :].bitcast(I32), tab_scales[0:2].rearrange("a q t -> (a q) t").bitcast(I32)
@@ -155,11 +162,9 @@ def tile_list_chess_feature_value_kernel(
 
         move_scales(moves[:6])
         raw_wp[0, 1] = load_wp(0, 1, AT_WP01)
-        move_scales(moves[6:8])
+        move_scales(moves[6:])
         picked = {}
         pick(0, table_0, AT_PICKED0)
-        picked_plane.append(slot([P, S], U8, "picked_plane2", AT_THREAT_PLANE))
-        nc.vector.memset(picked_plane[THREAT][:].bitcast(I32), 0)
         inverse = slot([P, 2 * PACK], F32, "inverse", AT_INVERSE)
         nc.vector.tensor_scalar(inverse[:], rough[:], 1e-30, None, ALU.max)
         nc.vector.reciprocal(inverse[:], inverse[:])
@@ -180,7 +185,6 @@ def tile_list_chess_feature_value_kernel(
 
         table_threat = load_table(THREAT, AT_THREAT)
         wt_raw = [load_wt(0, AT_WT0)]
-        move_scales(moves[8:])
 
         def round_weight(raw, name, shared, tag):
             dealt = slot([P, PACK * PASS], BF16, name, tag)
@@ -206,6 +210,21 @@ def tile_list_chess_feature_value_kernel(
                 woven[:].rearrange("p (c i j) -> p c j i", i=4, j=PACK), raw[:].rearrange("p j (c i) -> p c j i", i=4)
             )
             return woven
+
+        def round_columns(woven, half, raw):
+            nc.vector.tensor_copy(
+                woven[:, half * PACK * CHUNK : (half + 1) * PACK * CHUNK].rearrange("p (c i j) -> p c j i", i=4, j=PACK),
+                raw[:].rearrange("p j (c i) -> p c j i", i=4),
+            )
+
+        def sign_columns(signed, g, half, dealt):
+            runs = slice(half * P // 2, (half + 1) * P // 2)
+            nc.vector.tensor_tensor(
+                signed[:].rearrange("p (t m) j -> p t m j", t=PACK)[:, :, runs, :],
+                dealt[:].rearrange("p (m t j) -> p t m j", t=PACK, j=PACK)[:, :, runs, :],
+                signs[:, g : g + 1, :].unsqueeze(1).to_broadcast([P, PACK, P // 2, PACK]),
+                ALU.mult,
+            )
 
         def quantize_weight(dealt, name, parts, tags=None):
             tags = tags or (name + "_codes", name + "_plane")
@@ -276,7 +295,7 @@ def tile_list_chess_feature_value_kernel(
         h_codes = [keep.tile([P, S], U32, name="h_codes%d" % g, align_bytes=64) for g in range(2)]
         h_plane = [keep.tile([P, S], U8, name="h_plane%d" % g, align_bytes=64) for g in range(2)]
 
-        def finish_hidden(g, cols, rectified, tag=None):
+        def finish_hidden(g, cols, rectified, tag=None, on_vector=0):
             width = cols.stop - cols.start
             c0 = cols.start % BANK
             name = "hid%d_%d" % (g, cols.start)
@@ -284,12 +303,17 @@ def tile_list_chess_feature_value_kernel(
                 hidden = ring.tile([P, width, PACK], BF16, name=name, tag="hidden", bufs=7, align_bytes=64)
             else:
                 hidden = slot([P, width, PACK], BF16, name, tag)
+            split = width - on_vector
             nc.scalar.activation(
-                hidden[:].rearrange("p (c i) t -> p c t i", i=4),
-                rectified[:, :, c0 : c0 + width].rearrange("p t (c i) -> p c t i", i=4),
+                hidden[:, 0:split, :].rearrange("p (c i) t -> p c t i", i=4),
+                rectified[:, :, c0 : c0 + split].rearrange("p t (c i) -> p c t i", i=4),
                 ACT.Square,
             )
             return hidden
+
+        def square_rest(hidden, rectified, split):
+            values = rectified[:, :, split:].rearrange("p t (c i) -> p c t i", i=4)
+            nc.vector.tensor_tensor(hidden[:, split:, :].rearrange("p (c i) t -> p c t i", i=4), values, values, ALU.mult)
 
         def cap_hidden(g, hidden):
             nc.vector.tensor_tensor(
@@ -393,11 +417,14 @@ def tile_list_chess_feature_value_kernel(
             wt_scales_raw[:, 0, :].rearrange("p (g m t) -> p g m t", g=2, t=PACK),
         )
         wt_raw.append(load_wt(1, AT_WT1))
+        raw_w20 = [load_columns(0, AT_W20A)]
         raw_wp[1, 0] = load_wp(1, 0, AT_WP10)
-        raw_w2 = [load_weight(w2[0:PASS, :], "raw_w20", AT_W20)]
+        raw_w20.append(load_columns(1, AT_W20B))
         raw_wp[1, 1] = load_wp(1, 1, AT_WP11)
-        pick(THREAT, table_threat, "I", (CHUNK, CHUNK, BANK))
-        raw_w2.append(load_weight(w2[PASS : 2 * PASS, :], "raw_w21", AT_W21))
+        picked[THREAT] = slot([P, S], U32, "picked2", "I")
+        for c0, width in ((0, CHUNK), (CHUNK, CHUNK), (BANK, BANK)):
+            pick_part(THREAT, table_threat, c0, width)
+        raw_w21 = load_weight(w2[PASS : 2 * PASS, :], "raw_w21", AT_W21)
         deal_wt(0, wt_raw[0], slice(0, 2))
         deal_wt(0, wt_raw[0], slice(2, 4))
         deal_wt(1, wt_raw[1], slice(0, 4))
@@ -408,16 +435,20 @@ def tile_list_chess_feature_value_kernel(
         rect00 = ring.tile([P, PACK, BANK], F32, name="rect00", tag="rectified", bufs=3)
         for quarter in range(2):
             rectify_quarter(0, rect00, quarter, banks0[0])
+        dealt0 = slot([P, PACK * PASS], BF16, "w20", AT_THREAT + 12 * KIB)
+        round_columns(dealt0, 0, raw_w20[0])
+        signed0 = ring.tile([P, PASS, PACK], BF16, name="signed0", tag="signed", bufs=2, align_bytes=64)
+        sign_columns(signed0, 0, 0, dealt0)
         dealt = round_weight(raw_wp[1, 0], "wp10", False, AT_THREAT)
+        round_columns(dealt0, 1, raw_w20[1])
         wp1 = [quantize_weight(dealt, "wp10", 1)]
-        dealt0 = round_rows(raw_w2[0], "w20", AT_WP10)
-        signed0 = sign_weight(0, dealt0)
-        dealt11 = round_weight(raw_wp[1, 1], "wp11", False, AT_W20)
-        w2_mx = [quantize_weight(signed0, "w20", 1)]
+        sign_columns(signed0, 0, 1, dealt0)
+        dealt11 = round_weight(raw_wp[1, 1], "wp11", False, AT_W20B)
+        w2_mx = [quantize_weight(signed0[:].rearrange("p c j -> p (c j)"), "w20", 1)]
         wp1.append(quantize_weight(dealt11, "wp11", 1))
         h00 = finish_hidden(0, slice(0, 512), rect00, "F")
         rect01 = rectify(0, 1, banks0[1])
-        h01 = finish_hidden(0, slice(512, 1024), rect01, "G")
+        h01 = finish_hidden(0, slice(512, 1024), rect01, "G", 64)
         banks1 = []
         for half in range(2):
             banks1.append(open_banks(1, half))
@@ -426,10 +457,11 @@ def tile_list_chess_feature_value_kernel(
                 for a in order:
                     weights = None if a == THREAT else wp1[a]
                     first_pass(banks1[half][t][:], 1, t, half, a, weights, a == order[0], a == order[-1])
-        dealt1 = round_rows(raw_w2[1], "w21", AT_WP11 + 4 * KIB)
+        dealt1 = round_rows(raw_w21, "w21", AT_WP11 + 4 * KIB)
         h00 = cap_into(0, h00, "capped00", AT_WP11)
         signed1 = sign_weight(1, dealt1)
         quantize_hidden(0, slice(0, 512), h00)
+        square_rest(h01, rect01, BANK - 64)
         rect10 = rectify(1, 0, banks1[0])
         h10 = finish_hidden(1, c0, rect10)
         h11 = finish_hidden(1, c1, rect10)

@@ -32,7 +32,7 @@ AT_WT1 = 8 * KIB
 AT_W20A = 9 * KIB
 AT_WP10 = 13 * KIB
 AT_W20B = 21 * KIB
-AT_DIAGONAL = 24 * KIB - 256
+AT_WT_ROWS = 23 * KIB
 AT_WP00 = 24 * KIB
 AT_TABLE0 = 32 * KIB
 AT_INVERSE = 32 * KIB
@@ -90,13 +90,24 @@ def tile_list_chess_feature_value_kernel(
 
         offsets = keep.tile([P, S // 16], U16, name="offsets")
         nc.sync.dma_start(offsets[:], offs)
+        wt_rows = slot([P, 2, H], U8, "wt_rows", AT_WT_ROWS)
+        for half in range(2):
+            nc.sync.dma_start(
+                wt_rows[64 * half : 64 * half + 4, :, :].bitcast(I32),
+                wt_scales[0, 8 * half : 8 * half + 8, :].rearrange("(q r) c -> r q c", r=4).bitcast(I32),
+            )
         table_0 = load_table(0, AT_TABLE0)
         raw_wp = {}
 
         table_scales = slot([P, T], U8, "table_scales", AT_SCALES)
         nc.vector.memset(table_scales[:].bitcast(I32), 0)
-        wt_scales_raw = slot([P, 2, H], U8, "wt_scales_raw", "W")
-        nc.vector.memset(wt_scales_raw[:, 0, :].bitcast(I32), 0)
+        wt_scales_raw = keep.tile([P, H], U8, name="wt_scales_raw")
+        nc.vector.memset(wt_scales_raw[:].bitcast(I32), 0)
+        for q in range(4):
+            nc.vector.tensor_copy(
+                wt_scales_raw[32 * q : 32 * q + 4, :].bitcast(I32),
+                wt_rows[64 * (q // 2) : 64 * (q // 2) + 4, q % 2, :].bitcast(I32),
+            )
         picked_plane = [keep.tile([P, S], U8, name="picked_plane%d" % a, align_bytes=64) for a in range(3)]
         for a in range(3):
             nc.vector.memset(picked_plane[a][:].bitcast(I32), 0)
@@ -104,20 +115,13 @@ def tile_list_chess_feature_value_kernel(
             table_scales[0:P:4, :].bitcast(I32), tab_scales[0:2].rearrange("a q t -> (a q) t").bitcast(I32)
         )
         nc.sync.dma_start(table_scales[6:P:8, :].bitcast(I32), tab_scales[THREAT].bitcast(I32))
-        for half in range(2):
-            nc.sync.dma_start(
-                wt_scales_raw[64 * half : 64 * half + 4, :, :].bitcast(I32),
-                wt_scales[0, 8 * half : 8 * half + 8, :].rearrange("(q r) c -> r q c", r=4).bitcast(I32),
-            )
 
         rows_in = keep.tile([P, H], F32, name="rows_in")
         nc.gpsimd.memset(rows_in[:], 0.0)
         nc.scalar.dma_start(rows_in[GAIN_ROW : GAIN_ROW + 1, :], gain.unsqueeze(0))
         nc.scalar.dma_start(rows_in[BIAS_ROW : BIAS_ROW + 1, :], bh.unsqueeze(0))
         identity = keep.tile([P, P], F32, name="identity")
-        diagonal = slot([P, P], F32, "diagonal", AT_DIAGONAL)
-        make_identity(nc, diagonal[:])
-        nc.vector.tensor_copy(identity[:], diagonal[:])
+        make_identity(nc, identity[:])
         turned = keep.tile([P, 2, PACK, 2], F32, name="turned")
         for g in range(2):
             bank = psum.tile([P, PACK, P], F32, name="turn%d" % g, tag="bank%d" % g)
@@ -407,14 +411,9 @@ def tile_list_chess_feature_value_kernel(
         pick(1, table_1, "D")
         weights = quantize_weight(round_shared(raw_wp[0, 1], "wp01", "I"), "wp01", 2)
         group0_passes(banks0, 1, weights, False, False)
-        for half in range(2):
-            nc.vector.tensor_copy(
-                wt_scales_raw[64 * half + 32 : 64 * half + 36, 0, :].bitcast(I32),
-                wt_scales_raw[64 * half : 64 * half + 4, 1, :].bitcast(I32),
-            )
         nc.vector.tensor_copy(
             wt_plane[:].rearrange("p (g t m) -> p g m t", g=2, t=PACK),
-            wt_scales_raw[:, 0, :].rearrange("p (g m t) -> p g m t", g=2, t=PACK),
+            wt_scales_raw[:].rearrange("p (g m t) -> p g m t", g=2, t=PACK),
         )
         wt_raw.append(load_wt(1, AT_WT1))
         raw_w20 = [load_columns(0, AT_W20A)]

@@ -353,7 +353,7 @@ def tile_list_chess_feature_value_kernel(
         y_rows = out_0.rearrange("(p t) j -> p t j", t=PACK)
         y_words = out_1[0].rearrange("p m t -> p (m t)").bitcast(I32)
 
-        def second_stage(cols, w2_mx, first_bank, on_vector=0, into=None):
+        def second_stage(cols, w2_mx, first_bank, on_vector=0, into=None, by_bank=False):
             width = cols.stop - cols.start
             side = BANK // width
             banks = [
@@ -382,7 +382,10 @@ def tile_list_chess_feature_value_kernel(
                     nc.vector.tensor_copy(dst, banks[b][:])
                 else:
                     nc.scalar.copy(dst, banks[b][:])
-            nc.sync.dma_start(y_rows[:, :, cols], y[:])
+                if by_bank:
+                    nc.sync.dma_start(y_rows[:, b * side : (b + 1) * side, cols], y[:, b * side : (b + 1) * side, :])
+            if not by_bank:
+                nc.sync.dma_start(y_rows[:, :, cols], y[:])
             return y[:]
 
         def round_y(cols, y, copy=nc.vector.tensor_copy):
@@ -470,9 +473,9 @@ def tile_list_chess_feature_value_kernel(
         cap_hidden(1, h11)
         cap_hidden(0, h01)
         quantize_hidden(1, c1, h11)
+        y0 = second_stage(c0, w2_mx, 0, 2)
         quantize_hidden(0, slice(512, 1024), h01)
         rect11 = rectify(1, 1, banks1[1])
-        y0 = second_stage(c0, w2_mx, 0, 2)
         h12 = finish_hidden(1, c2, rect11)
         cap_hidden(1, h12)
         quantize_hidden(1, c2, h12)
@@ -486,7 +489,7 @@ def tile_list_chess_feature_value_kernel(
         r0 = round_y(c0, y0)
         r1 = round_y(c1, y1)
         quantize_y(c0, r0)
-        y2 = second_stage(c2, w2_mx, 4)
+        y2 = second_stage(c2, w2_mx, 4, by_bank=True)
         y_late = ring.tile([P, PACK, 256], F32, name="y_late", tag="y", bufs=4)
         y3 = second_stage(c3, w2_mx, 0, 0, y_late[:, :, 0:128])
         y4 = second_stage(c4, w2_mx, 1, 0, y_late[:, :, 128:256])
@@ -497,7 +500,7 @@ def tile_list_chess_feature_value_kernel(
         r3 = round_y(c3, y3)
         quantize_y(c2, r2)
         store_codes(c2)
-        r4 = round_y(c4, y4, nc.scalar.copy)
+        r4 = round_y(c4, y4)
         quantize_y(c3, r3)
         quantize_y(c4, r4)
         store_codes(late)

from contextlib import ExitStack

import concourse.mybir as mybir
from concourse.masks import make_identity

K, KP, KT, T, S, H, N = 1536, 1024, 512, 4096, 1024, 1024, 512
FLOPS = 2 * K * H * S + 2 * H * N * S

F32 = mybir.dt.float32
BF16 = mybir.dt.bfloat16
I32 = mybir.dt.int32
U32 = mybir.dt.uint32
U16 = mybir.dt.uint16
U8 = mybir.dt.uint8
E4M3 = mybir.dt.float8_e4m3fn_x4
E2M1 = mybir.dt.float4_e2m1fn_x4
ACT = mybir.ActivationFunctionType
ALU = mybir.AluOpType

P = 128
PACK = 4
PASS = P * PACK
BANK = 512
CHUNK = 256
THREAT = 2
SCALE_ROW = {THREAT: 0, 0: 4, 1: 8}
GAIN_ROW, BIAS_ROW = 16, 24
KIB = 1024
AT_WP11 = 0
AT_TABLE1 = 8 * KIB - 64
AT_WT1 = 8 * KIB
AT_W20A = 9 * KIB
AT_WP10 = 13 * KIB
AT_W20B = 21 * KIB
AT_WT_ROWS = 23 * KIB
AT_WP00 = 24 * KIB
AT_TABLE0 = 32 * KIB
AT_INVERSE = 32 * KIB
AT_WT0 = 32 * KIB + 64
AT_THREAT = 34 * KIB + 64
AT_W21 = 38 * KIB + 64
AT_PICKED0 = 50 * KIB + 64
AT_SCALES = 54 * KIB
AT_POSITIVE = 55 * KIB
AT_WP01 = 58 * KIB - 64


def tile_list_chess_feature_value_kernel(
    tc, tab_words, tab_scales, offs, wp, wt_words, wt_scales, bh, gain, w2, out_0, out_1, out_2
):
    nc = tc.nc
    with ExitStack() as ctx:
        keep = ctx.enter_context(tc.tile_pool(name="keep", bufs=1))
        ring = ctx.enter_context(tc.tile_pool(name="ring", bufs=1))
        lap = ctx.enter_context(tc.tile_pool(name="lap", bufs=1))
        psum = ctx.enter_context(tc.psum_pool(name="psum", bufs=1))

        def slot(shape, dtype, name, tag):
            if isinstance(tag, int):
                return lap.tile(shape, dtype, name=name, offset=tag, align_bytes=64)
            return ring.tile(shape, dtype, name=name, tag=tag, bufs=1, align_bytes=64)

        def load_table(a, tag):
            words = slot([P, T], U32, "table%d" % a, tag)
            nc.sync.dma_start(words[:].bitcast(I32), tab_words[a].rearrange("p t i -> p (t i)").bitcast(I32))
            return words

        def load_weight(rows, name, tag):
            raw = slot([P, PACK, PASS], F32, name, tag)
            nc.sync.dma_start(raw[:], rows.rearrange("(p j) c -> p j c", j=PACK))
            return raw

        def load_wp(g, a, tag):
            return load_weight(wp[a * PASS : (a + 1) * PASS, g * PASS : (g + 1) * PASS], "raw_wp%d%d" % (g, a), tag)

        def pick_part(a, words, c0, width):
            nc.vector.tensor_copy(
                picked[a][:, c0 : c0 + width], words[:].indirect(offsets[:, c0 // 16 : (c0 + width) // 16])
            )

        def pick(a, words, tag):
            picked[a] = slot([P, S], U32, "picked%d" % a, tag)
            pick_part(a, words, 0, S)

        def load_columns(half, tag):
            raw = slot([P, PACK, CHUNK], F32, "raw_w20%d" % half, tag)
            rows = w2[0:PASS, half * CHUNK : (half + 1) * CHUNK]
            nc.sync.dma_start(raw[:], rows.rearrange("(p j) c -> p j c", j=PACK))
            return raw

        offsets = keep.tile([P, S // 16], U16, name="offsets")
        nc.sync.dma_start(offsets[:], offs)
        wt_rows = slot([P, 2, H], U8, "wt_rows", AT_WT_ROWS)
        for half in range(2):
            nc.sync.dma_start(
                wt_rows[64 * half : 64 * half + 4, :, :].bitcast(I32),
                wt_scales[0, 8 * half : 8 * half + 8, :].rearrange("(q r) c -> r q c", r=4).bitcast(I32),
            )
        table_0 = load_table(0, AT_TABLE0)
        raw_wp = {}

        table_scales = slot([P, T], U8, "table_scales", AT_SCALES)
        nc.vector.memset(table_scales[:].bitcast(I32), 0)
        wt_scales_raw = keep.tile([P, H], U8, name="wt_scales_raw")
        nc.vector.memset(wt_scales_raw[:].bitcast(I32), 0)
        for q in range(4):
            nc.vector.tensor_copy(
                wt_scales_raw[32 * q : 32 * q + 4, :].bitcast(I32),
                wt_rows[64 * (q // 2) : 64 * (q // 2) + 4, q % 2, :].bitcast(I32),
            )
        picked_plane = [keep.tile([P, S], U8, name="picked_plane%d" % a, align_bytes=64) for a in range(3)]
        for a in range(3):
            nc.vector.memset(picked_plane[a][:].bitcast(I32), 0)
        nc.sync.dma_start(
            table_scales[0:P:4, :].bitcast(I32), tab_scales[0:2].rearrange("a q t -> (a q) t").bitcast(I32)
        )
        nc.sync.dma_start(table_scales[6:P:8, :].bitcast(I32), tab_scales[THREAT].bitcast(I32))

        rows_in = keep.tile([P, H], F32, name="rows_in")
        nc.gpsimd.memset(rows_in[:], 0.0)
        nc.scalar.dma_start(rows_in[GAIN_ROW : GAIN_ROW + 1, :], gain.unsqueeze(0))
        nc.scalar.dma_start(rows_in[BIAS_ROW : BIAS_ROW + 1, :], bh.unsqueeze(0))
        identity = keep.tile([P, P], F32, name="identity")
        make_identity(nc, identity[:])
        turned = keep.tile([P, 2, PACK, 2], F32, name="turned")
        for g in range(2):
            bank = psum.tile([P, PACK, P], F32, name="turn%d" % g, tag="bank%d" % g)
            for t in range(PACK):
                nc.tensor.transpose(bank[:, t, :], rows_in[:, g * PASS + t : (g + 1) * PASS : PACK], identity[:])
            nc.scalar.copy(turned[:, g, :, :], bank[:, :, GAIN_ROW : BIAS_ROW + 1 : BIAS_ROW - GAIN_ROW])
        gains = turned[:, :, :, 0]
        bias = turned[:, :, :, 1]

        wt_dealt = [keep.tile([P, H], U8, name="wt_dealt%d" % g, align_bytes=64) for g in range(2)]
        wt_plane = keep.tile([P, H], U8, name="wt_plane", align_bytes=64)

        raw_wp[0, 0] = load_wp(0, 0, AT_WP00)
        table_1 = load_table(1, AT_TABLE1)

        picked_scales = keep.tile([P, S], U8, name="picked_scales", align_bytes=64)
        nc.vector.tensor_copy(picked_scales[:], table_scales[:].indirect(offsets[:]))
        magnitude = keep.tile([P, 2 * PACK], F32, name="magnitude")
        nc.scalar.activation(magnitude[:].rearrange("p (g t) -> p g t", g=2), gains, ACT.Abs)
        rough = keep.tile([P, 2 * PACK], F32, name="rough")
        nc.scalar.activation(rough[:], magnitude[:], ACT.Sqrt)
        moves = [(a, r) for a in (0, 1, THREAT) for r in range(4)]

        def move_scales(some):
            for a, r in some:
                rows = slice(6 + 8 * r, P, 32) if a == THREAT else slice(64 * a + 4 * r, 64 * (a + 1), 16)
                nc.sync.dma_start(
                    picked_plane[a][SCALE_ROW[a] + r : P : 32, :].bitcast(I32),
                    picked_scales[rows, :].bitcast(I32),
                )

        def load_wt(g, tag):
            raw = slot([P, H], U8, "wt_raw%d" % g, tag)
            nc.sync.dma_start(raw[:].bitcast(I32), wt_words[0][:, g * H : (g + 1) * H].bitcast(I32))
            return raw

        def deal_wt(g, raw, tiles):
            nc.scalar.copy(
                wt_dealt[g][:].bitcast(U16).rearrange("p (t m) -> p m t", t=PACK)[:, :, tiles],
                raw[:].bitcast(U16).rearrange("p (m t) -> p m t", t=PACK)[:, :, tiles],
            )

        move_scales(moves[:6])
        raw_wp[0, 1] = load_wp(0, 1, AT_WP01)
        move_scales(moves[6:])
        picked = {}
        pick(0, table_0, AT_PICKED0)
        inverse = slot([P, 2 * PACK], F32, "inverse", AT_INVERSE)
        nc.vector.tensor_scalar(inverse[:], rough[:], 1e-30, None, ALU.max)
        nc.vector.reciprocal(inverse[:], inverse[:])
        nc.vector.tensor_tensor(inverse[:], inverse[:], magnitude[:], ALU.mult)
        nc.vector.tensor_tensor(inverse[:], inverse[:], rough[:], ALU.add)
        root = keep.tile([P, 2 * PACK], F32, name="root")
        nc.vector.tensor_scalar(root[:], inverse[:], 0.5, None, ALU.mult)
        root_bias = keep.tile([P, 2 * PACK], F32, name="root_bias")
        nc.vector.tensor_tensor(
            root_bias[:].rearrange("p (g t) -> p g t", g=2), root[:].rearrange("p (g t) -> p g t", g=2), bias, ALU.mult
        )
        ceiling = keep.tile([P, 2, PACK], BF16, name="ceiling")
        nc.vector.tensor_copy(ceiling[:].rearrange("p g t -> p (g t)"), magnitude[:])
        positive = slot([P, 2, PACK], F32, "positive", AT_POSITIVE)
        nc.vector.tensor_scalar(positive[:], gains, 0.0, None, ALU.is_ge)
        signs = keep.tile([P, 2, PACK], BF16, name="signs")
        nc.vector.tensor_scalar(signs[:], positive[:], 2.0, -1.0, ALU.mult, ALU.add)

        table_threat = load_table(THREAT, AT_THREAT)
        wt_raw = [load_wt(0, AT_WT0)]

        def round_weight(raw, name, shared, tag):
            dealt = slot([P, PACK * PASS], BF16, name, tag)
            dst = dealt[:].rearrange("p (t m j) -> p m j t", t=PACK, j=PACK)
            src = raw[:].rearrange("p j (m t) -> p m j t", t=PACK)
            if shared:
                nc.scalar.copy(dst, src)
            else:
                nc.vector.tensor_copy(dst, src)
            return dealt

        def round_shared(raw, name, tag):
            dealt = slot([P, PACK * PASS], BF16, name, tag)
            dst = dealt[:].rearrange("p (t m j) -> p m j t", t=PACK, j=PACK)
            src = raw[:].rearrange("p j (m t) -> p m j t", t=PACK)
            nc.vector.tensor_copy(dst[:, :, :, 0:2], src[:, :, :, 0:2])
            nc.scalar.copy(dst[:, :, :, 2:4], src[:, :, :, 2:4])
            return dealt

        def round_rows(raw, name, tag):
            woven = slot([P, PACK * PASS], BF16, name, tag)
            nc.vector.tensor_copy(
                woven[:].rearrange("p (c i j) -> p c j i", i=4, j=PACK), raw[:].rearrange("p j (c i) -> p c j i", i=4)
            )
            return woven

        def round_columns(woven, half, raw):
            nc.vector.tensor_copy(
                woven[:, half * PACK * CHUNK : (half + 1) * PACK * CHUNK].rearrange("p (c i j) -> p c j i", i=4, j=PACK),
                raw[:].rearrange("p j (c i) -> p c j i", i=4),
            )

        def sign_columns(signed, g, half, dealt):
            runs = slice(half * P // 2, (half + 1) * P // 2)
            nc.vector.tensor_tensor(
                signed[:].rearrange("p (t m) j -> p t m j", t=PACK)[:, :, runs, :],
                dealt[:].rearrange("p (m t j) -> p t m j", t=PACK, j=PACK)[:, :, runs, :],
                signs[:, g : g + 1, :].unsqueeze(1).to_broadcast([P, PACK, P // 2, PACK]),
                ALU.mult,
            )

        def quantize_weight(dealt, name, parts, tags=None):
            tags = tags or (name + "_codes", name + "_plane")
            codes = slot([P, PASS], U32, name + "_codes", tags[0])
            plane = slot([P, PASS], U8, name + "_plane", tags[1])
            width = PASS // parts
            for part in range(parts):
                cols = slice(part * width, (part + 1) * width)
                nc.vector.quantize_mx(
                    out=codes[:, cols].bitcast(E4M3),
                    scales=plane[:, cols],
                    in_=dealt[:, PACK * cols.start : PACK * cols.stop],
                )
            return codes, plane

        def first_pass(bank, g, t, half, a, weights, start, stop, cols=None):
            cols = cols or slice(half * BANK, (half + 1) * BANK)
            if a == THREAT:
                c0 = g * PASS + t * P
                lhs = wt_dealt[g][:, 2 * t * P : 2 * (t + 1) * P].bitcast(E2M1)
                lhs_scale = wt_plane[:, c0 : c0 + P]
            else:
                codes, plane = weights
                lhs = codes[:, t * P : (t + 1) * P].bitcast(E4M3)
                lhs_scale = plane[:, t * P : (t + 1) * P]
            nc.tensor.matmul_mx(
                out=bank,
                lhsT=lhs,
                lhsT_scale=lhs_scale,
                rhs=picked[a][:, cols].bitcast(E4M3),
                rhs_scale=picked_plane[a][SCALE_ROW[a] :, cols],
                start=start,
                stop=stop,
            )

        def quartered_pass(banks, g, half, quarter, t, a, weights, first, last):
            c0 = half * BANK + quarter * CHUNK
            out = banks[2 * quarter + t // 2][:, (t % 2) * CHUNK : (t % 2 + 1) * CHUNK]
            first_pass(out, g, t, half, a, weights, first and t % 2 == 0, last and t % 2 == 1, slice(c0, c0 + CHUNK))

        def group0_passes(banks0, a, weights, first, last):
            for quarter in range(2):
                for t in range(PACK):
                    quartered_pass(banks0[0], 0, 0, quarter, t, a, weights, first, last)
            for t in range(PACK):
                first_pass(banks0[1][t][:], 0, t, 1, a, weights, first, last)

        def rectify(g, half, banks):
            rectified = ring.tile([P, PACK, BANK], F32, name="rect%d%d" % (g, half), tag="rectified", bufs=3)
            for t in range(PACK):
                column = slice(g * PACK + t, g * PACK + t + 1)
                nc.scalar.activation(
                    rectified[:, t, :], banks[t][:], ACT.Relu, bias=root_bias[:, column], scale=root[:, column]
                )
            return rectified

        def rectify_quarter(g, rectified, quarter, banks):
            for t in range(PACK):
                column = slice(g * PACK + t, g * PACK + t + 1)
                nc.scalar.activation(
                    rectified[:, t, quarter * CHUNK : (quarter + 1) * CHUNK],
                    banks[2 * quarter + t // 2][:, (t % 2) * CHUNK : (t % 2 + 1) * CHUNK],
                    ACT.Relu,
                    bias=root_bias[:, column],
                    scale=root[:, column],
                )

        h_codes = [keep.tile([P, S], U32, name="h_codes%d" % g, align_bytes=64) for g in range(2)]
        h_plane = [keep.tile([P, S], U8, name="h_plane%d" % g, align_bytes=64) for g in range(2)]

        def finish_hidden(g, cols, rectified, tag=None, on_vector=0):
            width = cols.stop - cols.start
            c0 = cols.start % BANK
            name = "hid%d_%d" % (g, cols.start)
            if tag is None:
                hidden = ring.tile([P, width, PACK], BF16, name=name, tag="hidden", bufs=7, align_bytes=64)
            else:
                hidden = slot([P, width, PACK], BF16, name, tag)
            split = width - on_vector
            nc.scalar.activation(
                hidden[:, 0:split, :].rearrange("p (c i) t -> p c t i", i=4),
                rectified[:, :, c0 : c0 + split].rearrange("p t (c i) -> p c t i", i=4),
                ACT.Square,
            )
            return hidden

        def square_rest(hidden, rectified, split):
            values = rectified[:, :, split:].rearrange("p t (c i) -> p c t i", i=4)
            nc.vector.tensor_tensor(hidden[:, split:, :].rearrange("p (c i) t -> p c t i", i=4), values, values, ALU.mult)

        def cap_hidden(g, hidden):
            nc.vector.tensor_tensor(
                hidden[:], hidden[:], ceiling[:, g : g + 1, :].to_broadcast(list(hidden.shape)), ALU.min
            )

        def cap_into(g, hidden, name, tag):
            capped = slot(list(hidden.shape), BF16, name, tag)
            nc.vector.tensor_tensor(
                capped[:], hidden[:], ceiling[:, g : g + 1, :].to_broadcast(list(hidden.shape)), ALU.min
            )
            return capped

        def sign_weight(g, dealt):
            signed = ring.tile([P, PASS, PACK], BF16, name="signed%d" % g, tag="signed", bufs=2, align_bytes=64)
            nc.vector.tensor_tensor(
                signed[:].rearrange("p (t m) j -> p t m j", t=PACK),
                dealt[:].rearrange("p (m t j) -> p t m j", t=PACK, j=PACK),
                signs[:, g : g + 1, :].unsqueeze(1).to_broadcast([P, PACK, P, PACK]),
                ALU.mult,
            )
            return signed[:].rearrange("p c j -> p (c j)")

        def quantize_hidden(g, cols, hidden):
            nc.vector.quantize_mx(
                out=h_codes[g][:, cols].bitcast(E4M3),
                scales=h_plane[g][:, cols],
                in_=hidden[:].rearrange("p n t -> p (n t)"),
            )

        y_codes = keep.tile([P, S], U32, name="y_codes", align_bytes=64)
        y_plane = keep.tile([P, S], U8, name="y_plane", align_bytes=64)
        y_rows = out_0.rearrange("(p t) j -> p t j", t=PACK)
        y_words = out_1[0].rearrange("p m t -> p (m t)").bitcast(I32)

        def second_stage(cols, w2_mx, first_bank, on_vector=0, into=None, by_bank=False):
            width = cols.stop - cols.start
            side = BANK // width
            banks = [
                psum.tile([P, BANK], F32, name="ybank%d_%d" % (cols.start, b), tag="bank%d" % (first_bank + b))
                for b in range(PACK // side)
            ]
            for g in range(2):
                codes, plane = w2_mx[g]
                for t in range(PACK):
                    nc.tensor.matmul_mx(
                        out=banks[t // side][:, (t % side) * width : (t % side + 1) * width],
                        lhsT=codes[:, t * P : (t + 1) * P].bitcast(E4M3),
                        lhsT_scale=plane[:, t * P : (t + 1) * P],
                        rhs=h_codes[g][:, cols].bitcast(E4M3),
                        rhs_scale=h_plane[g][:, cols],
                        start=(g == 0 and t % side == 0),
                        stop=(g == 1 and t % side == side - 1),
                    )
            if into is not None:
                nc.scalar.copy(into, banks[0][:].rearrange("p (t n) -> p t n", t=PACK))
                return into
            y = ring.tile([P, PACK, width], F32, name="y%d" % cols.start, tag="y", bufs=4)
            for b in range(PACK // side):
                dst = y[:, b * side : (b + 1) * side, :].rearrange("p t n -> p (t n)")
                if b >= len(banks) - on_vector:
                    nc.vector.tensor_copy(dst, banks[b][:])
                else:
                    nc.scalar.copy(dst, banks[b][:])
                if by_bank:
                    nc.sync.dma_start(y_rows[:, b * side : (b + 1) * side, cols], y[:, b * side : (b + 1) * side, :])
            if not by_bank:
                nc.sync.dma_start(y_rows[:, :, cols], y[:])
            return y[:]

        def round_y(cols, y, copy=nc.vector.tensor_copy):
            width = cols.stop - cols.start
            rounded = ring.tile([P, width, PACK], BF16, name="yb%d" % cols.start, tag="rounded", bufs=3, align_bytes=64)
            copy(rounded[:].rearrange("p (c i) t -> p c t i", i=4), y.rearrange("p t (c i) -> p c t i", i=4))
            return rounded

        def quantize_y(cols, rounded):
            nc.vector.quantize_mx(
                out=y_codes[:, cols].bitcast(E4M3), scales=y_plane[:, cols], in_=rounded[:].rearrange("p n t -> p (n t)")
            )

        def store_codes(cols):
            nc.sync.dma_start(y_words[:, cols], y_codes[:, cols].bitcast(I32))

        def open_banks(g, half):
            return [
                psum.tile([P, BANK], F32, name="bank%d%d%d" % (g, half, t), tag="bank%d" % (PACK * half + t))
                for t in range(PACK)
            ]

        banks0 = [open_banks(0, half) for half in range(2)]
        weights = quantize_weight(round_weight(raw_wp[0, 0], "wp00", True, "H"), "wp00", 1)
        group0_passes(banks0, 0, weights, True, False)
        pick(1, table_1, "D")
        weights = quantize_weight(round_shared(raw_wp[0, 1], "wp01", "I"), "wp01", 2)
        group0_passes(banks0, 1, weights, False, False)
        nc.vector.tensor_copy(
            wt_plane[:].rearrange("p (g t m) -> p g m t", g=2, t=PACK),
            wt_scales_raw[:].rearrange("p (g m t) -> p g m t", g=2, t=PACK),
        )
        wt_raw.append(load_wt(1, AT_WT1))
        raw_w20 = [load_columns(0, AT_W20A)]
        raw_wp[1, 0] = load_wp(1, 0, AT_WP10)
        raw_w20.append(load_columns(1, AT_W20B))
        raw_wp[1, 1] = load_wp(1, 1, AT_WP11)
        picked[THREAT] = slot([P, S], U32, "picked2", "I")
        for c0, width in ((0, CHUNK), (CHUNK, CHUNK), (BANK, BANK)):
            pick_part(THREAT, table_threat, c0, width)
        raw_w21 = load_weight(w2[PASS : 2 * PASS, :], "raw_w21", AT_W21)
        deal_wt(0, wt_raw[0], slice(0, 2))
        deal_wt(0, wt_raw[0], slice(2, 4))
        deal_wt(1, wt_raw[1], slice(0, 4))
        group0_passes(banks0, THREAT, None, False, True)
        chunks = [slice(0, 256), slice(256, 512), slice(512, 768), slice(768, 896), slice(896, 1024)]
        c0, c1, c2, c3, c4 = chunks
        late = slice(768, 1024)
        rect00 = ring.tile([P, PACK, BANK], F32, name="rect00", tag="rectified", bufs=3)
        for quarter in range(2):
            rectify_quarter(0, rect00, quarter, banks0[0])
        dealt0 = slot([P, PACK * PASS], BF16, "w20", AT_THREAT + 12 * KIB)
        round_columns(dealt0, 0, raw_w20[0])
        signed0 = ring.tile([P, PASS, PACK], BF16, name="signed0", tag="signed", bufs=2, align_bytes=64)
        sign_columns(signed0, 0, 0, dealt0)
        dealt = round_weight(raw_wp[1, 0], "wp10", False, AT_THREAT)
        round_columns(dealt0, 1, raw_w20[1])
        wp1 = [quantize_weight(dealt, "wp10", 1)]
        sign_columns(signed0, 0, 1, dealt0)
        dealt11 = round_weight(raw_wp[1, 1], "wp11", False, AT_W20B)
        w2_mx = [quantize_weight(signed0[:].rearrange("p c j -> p (c j)"), "w20", 1)]
        wp1.append(quantize_weight(dealt11, "wp11", 1))
        h00 = finish_hidden(0, slice(0, 512), rect00, "F")
        rect01 = rectify(0, 1, banks0[1])
        h01 = finish_hidden(0, slice(512, 1024), rect01, "G", 64)
        banks1 = []
        for half in range(2):
            banks1.append(open_banks(1, half))
            for t in range(PACK):
                order = (1, THREAT, 0) if half and t >= 2 else (THREAT, 0, 1)
                for a in order:
                    weights = None if a == THREAT else wp1[a]
                    first_pass(banks1[half][t][:], 1, t, half, a, weights, a == order[0], a == order[-1])
        dealt1 = round_rows(raw_w21, "w21", AT_WP11 + 4 * KIB)
        h00 = cap_into(0, h00, "capped00", AT_WP11)
        signed1 = sign_weight(1, dealt1)
        quantize_hidden(0, slice(0, 512), h00)
        square_rest(h01, rect01, BANK - 64)
        rect10 = rectify(1, 0, banks1[0])
        h10 = finish_hidden(1, c0, rect10)
        h11 = finish_hidden(1, c1, rect10)
        cap_hidden(1, h10)
        w2_mx.append(quantize_weight(signed1, "w21", 1))
        quantize_hidden(1, c0, h10)
        cap_hidden(1, h11)
        cap_hidden(0, h01)
        quantize_hidden(1, c1, h11)
        y0 = second_stage(c0, w2_mx, 0, 2)
        quantize_hidden(0, slice(512, 1024), h01)
        rect11 = rectify(1, 1, banks1[1])
        h12 = finish_hidden(1, c2, rect11)
        cap_hidden(1, h12)
        quantize_hidden(1, c2, h12)
        y1 = second_stage(c1, w2_mx, 2)
        h13 = finish_hidden(1, c3, rect11)
        cap_hidden(1, h13)
        quantize_hidden(1, c3, h13)
        h14 = finish_hidden(1, c4, rect11)
        cap_hidden(1, h14)
        quantize_hidden(1, c4, h14)
        r0 = round_y(c0, y0)
        r1 = round_y(c1, y1)
        quantize_y(c0, r0)
        y2 = second_stage(c2, w2_mx, 4, by_bank=True)
        y_late = ring.tile([P, PACK, 256], F32, name="y_late", tag="y", bufs=4)
        y3 = second_stage(c3, w2_mx, 0, 0, y_late[:, :, 0:128])
        y4 = second_stage(c4, w2_mx, 1, 0, y_late[:, :, 128:256])
        nc.sync.dma_start(y_rows[:, :, late], y_late[:])
        quantize_y(c1, r1)
        store_codes(slice(0, 512))
        r2 = round_y(c2, y2)
        r3 = round_y(c3, y3)
        quantize_y(c2, r2)
        store_codes(c2)
        r4 = round_y(c4, y4)
        quantize_y(c3, r3)
        quantize_y(c4, r4)
        store_codes(late)
        for q in range(4):
            (nc.sync if q < 2 else nc.scalar).dma_start(
                out_2[0, 4 * q : 4 * q + 4, :].bitcast(I32), y_plane[32 * q : 32 * q + 4, :].bitcast(I32)
            )
